import numpy as np, ml_dtypes
CORES = [10,34,74,98]
N = 4
BF = ml_dtypes.bfloat16
def gentries(a):
    return np.ascontiguousarray(a.reshape(8, 16, -1).transpose(0, 2, 1)).reshape(8, -1)
def gtable(e):
    e = np.asarray(e); return np.ascontiguousarray(e.reshape(8, -1, 16).transpose(0, 2, 1)).reshape(128, -1).astype(np.int32)
def f(rng, *shape):
    return (rng.standard_normal(shape, dtype=np.float32) * np.exp2(rng.integers(-2, 3, shape[:-1] + (1,)))).astype(BF)
def wide(rng, *shape):
    v = f(rng, *shape).astype(np.float32); k = shape[:-2] + (1, shape[-1])
    return (v * np.exp2(rng.integers(-6, 7, k)) * (rng.random(k) > 0.0625)).astype(BF)
R, G, NT, E, RD = 1024, 256, 512, 4, 4
H, W = R // 2, R + N * G
def energies(rng, n):
    v = rng.standard_normal((N, 8, 16, n), dtype=np.float32) * np.exp2(rng.integers(-1, 2, (N, 8, 1, 1))).astype(np.float32)
    return v.reshape(N, 128, n).astype(BF)
def glist(e):
    return np.stack([gtable(v) for v in e])
def ungl(a):
    return np.stack([gentries(v) for v in a]).astype(np.int64)
def setup_inputs(rng):
    return {"own": energies(rng, R), "pair": energies(rng, 16 * NT), "st": rng.integers(0, 16, (N, 8, R)).astype(np.int32),
            "nb": glist(rng.integers(0, W, (N, 8, E * R))), "th": glist(rng.integers(0, W, (N, 8, E * R))), "tb": glist(rng.integers(0, NT, (N, 8, E * R))),
            "sd": glist(rng.integers(0, R, (N, 8, N * G)))}
def setup_inputs_ties(rng):
    d = setup_inputs(rng)
    own = rng.integers(0, 2, (N, 128, R)).astype(np.float32); pair = rng.integers(0, 3, (N, 128, 16 * NT)).astype(np.float32)
    q, g = int(rng.integers(0, N)), int(rng.integers(0, 8)); own[q, 16 * g:16 * g + 16] = 0; pair[q, 16 * g:16 * g + 16] = 0
    d["own"] = own.astype(BF); d["pair"] = pair.astype(BF); return d
def setup_inputs_ends(rng):
    d = setup_inputs(rng); v = np.array([0, H - 1, H, R - 1, R, R + G - 1, R + G, W - G, W - 1])
    d["nb"] = glist(rng.choice(v, (N, 8, E * R))); d["th"] = glist(rng.choice(v, (N, 8, E * R)))
    d["tb"] = glist(rng.choice(np.array([0, 1, NT - 2, NT - 1]), (N, 8, E * R))); d["sd"] = glist(rng.choice(np.array([0, H - 1, H, R - 1]), (N, 8, N * G)))
    d["st"] = rng.choice(np.array([0, 15]), (N, 8, R)).astype(np.int32)
    o = d["own"].astype(np.float32).reshape(N, 8, 16, R); o[:, :, 1:15] += 96; d["own"] = o.reshape(N, 128, R).astype(BF); return d
def setup_inputs_far(rng):
    d = setup_inputs(rng); q = (np.arange(N)[:, None, None] + 1 + np.arange(8)[None, :, None] % (N - 1)) % N
    m = np.tile(np.arange(E * R) % G, (N, 8, 1))
    d["nb"] = glist(R + G * q + rng.permuted(m, axis=2)); d["th"] = glist(R + G * q + rng.permuted(m, axis=2))
    d["sd"] = glist(rng.permuted(np.tile(np.arange(R), (N, 8, N, 1)), axis=3)[..., :G].reshape(N, 8, N * G))
    big = rng.random((N, 8, 1, 1)) < 0.5; b, g = int(rng.integers(0, N)), int(rng.integers(0, 8)); big[b, g] = True
    z = np.where(big, 2.0 ** 32, 1.0).astype(np.float32)
    o = d["own"].astype(np.float32).reshape(N, 8, 16, R); o[b, g] = np.abs(o[b, g]) + 64
    d["own"] = (o * z).reshape(N, 128, R).astype(BF)
    d["pair"] = (d["pair"].astype(np.float32).reshape(N, 8, 16, 16 * NT) * z).reshape(N, 128, 16 * NT).astype(BF); return d
def setup_inputs_alike(rng):
    d = setup_inputs(rng)
    for k, top in (("nb", W), ("th", W), ("tb", NT)):
        d[k] = glist(np.repeat(rng.integers(0, top, (N, 8, 2 * E)), H, axis=2))
    d["sd"] = glist(np.repeat(rng.integers(0, R, (N, 8, N)), G, axis=2))
    d["pair"] = (d["pair"].astype(np.float32) * np.float32(0.25)).astype(BF); return d
def setup_inputs_spread(rng):
    d = setup_inputs(rng); d["own"] = wide(rng, N, 128, R); d["pair"] = wide(rng, N, 128, 16 * NT); return d
def check_inputs(d):
    bad = []
    for k, top in (("nb", W), ("th", W), ("tb", NT), ("sd", R), ("st", 16)):
        if np.min(d[k]) < 0 or np.max(d[k]) >= top:
            bad.append(k)
    for k in ("own", "pair"):
        v = np.abs(d[k].astype(np.float32))
        if not np.all((v == 0) | ((v >= 2.0 ** -60) & (v <= 2.0 ** 40))):
            bad.append(k)
    return bad
def reference(own, pair, st, nb, th, tb, sd):
    a = own.astype(np.float32).reshape(N, 8, 16, R); p = pair.astype(np.float32).reshape(N, 8, 16, 16 * NT)
    s = st.astype(np.int64); low = np.zeros((N, 8, R), np.float32)
    near, third, base = [ungl(v).reshape(N, 8, 2, E * H) for v in (nb, th, tb)]; listed = ungl(sd)
    for t in range(RD):
        h = t & 1
        sent = np.take_along_axis(s, listed, 2).reshape(N, 8, N, G)
        w = np.concatenate([s, sent.transpose(2, 1, 0, 3).reshape(N, 8, N * G)], 2)
        col = 16 * ((base[:, :, h] + 37 * np.take_along_axis(w, third[:, :, h], 2)) & (NT - 1)) + np.take_along_axis(w, near[:, :, h], 2)
        x = np.take_along_axis(p, col[:, :, None, :], 3)
        v = a[:, :, :, h * H:(h + 1) * H]
        for k in range(E):
            v = v + x[:, :, :, k * H:(k + 1) * H]
        s[:, :, h * H:(h + 1) * H] = np.argmin(v, 2)
        low[:, :, h * H:(h + 1) * H] = np.min(v, 2)
    return {"y": s.astype(np.float32), "e": low}

@@ -1,0 +1,353 @@
+from concourse.bass import DstId, RemoteDMATransfer
+from concourse.mybir import AluOpType, ActivationFunctionType
+
+BF, F32, I32, U16 = "bfloat16", "float32", "int32", "uint16"
+SCRATCH = {
+    "stc": ("sbuf", [128, 64], I32), "stb": ("sbuf", [128, 64], BF),
+    "sdr": ("sbuf", [128, 64], I32), "sdo": ("sbuf", [128, 64], U16),
+    "thr": ("sbuf", [128, 8, 32], I32), "nbr": ("sbuf", [128, 8, 32], I32), "tbr": ("sbuf", [128, 8, 32], I32),
+    "tho": ("sbuf", [128, 256], U16), "nbo": ("sbuf", [128, 256], U16), "tbf": ("sbuf", [128, 256], F32),
+    "ownb": ("sbuf", [128, 1024], BF), "pairb": ("sbuf", [128, 8192], BF),
+    "W": ("sbuf", [128, 2048], BF),
+    "xth": ("sbuf", [128, 2048], BF), "xnb": ("sbuf", [128, 2048], BF), "xp": ("sbuf", [128, 2048], BF),
+    "xs": ("sbuf", [128, 1024], BF),
+    "ia": ("sbuf", [128, 128], I32), "ib": ("sbuf", [128, 128], I32), "po": ("sbuf", [128, 128], U16),
+    "mb": ("sbuf", [128, 520], F32), "nd": ("sbuf", [128, 512], BF), "cb": ("sbuf", [128, 512], BF),
+    "snd": ("sbuf", [128, 192], BF), "lnd": ("sbuf", [128, 192], BF), "pad": ("sbuf", [128, 768], BF),
+    "ones": ("sbuf", [128, 144], BF), "band": ("sbuf", [128, 144], BF), "idf": ("sbuf", [128, 128], F32),
+    "dz": ("sbuf", [128, 144], BF), "du": ("sbuf", [128, 144], BF),
+    "pat": ("sbuf", [128, 256], BF), "rst": ("sbuf", [128, 256], F32),
+    "ysb": ("sbuf", [128, 1024], F32), "esb": ("sbuf", [128, 1024], F32),
+    "px0": ("psum", [128, 512], F32), "px1": ("psum", [128, 512], F32),
+    "pa0": ("psum", [128, 512], F32), "pa1": ("psum", [128, 512], F32), "pa2": ("psum", [128, 512], F32),
+    "pc": ("psum", [128, 512], F32),
+    "pra": ("psum", [128, 1024], BF), "prb": ("psum", [128, 1024], BF),
+}
+ROUNDS = 4
+DMAS = ["d_st", "d_sd", "d_th", "d_nb", "d_tb", "d_own", "d_p0", "d_p1", "d_y0", "d_y1", "d_e0", "d_e1"]
+SEMAPHORES = ["pe", "ve", "ac", "gp"] + DMAS + ["%s%d%d" % (n, x, k) for n in ("arr", "loc") for x in range(ROUNDS) for k in range(3)]
+BANKS = [n for n in SCRATCH if SCRATCH[n][0] == "psum"]
+BIG = float(2 ** 90)
+CFG = {"gam": 1.6e-3, "cyc": 1.04e-3, "pe": 0.52e-3, "hop": 0.1, "rows": 0.7, "lat": 1.8, "first": 3.0, "delta": 0.4,
+       "s1": (512, 512, 512, 512), "s2": (256, 128, 256, 256), "calls": ((0,), (1,), (2,)), "split": 3584,
+       "low": ((0, 2), (2, 1), (3, 1)), "pri": {"ia0": 2.0, "xp1536": 0.5, "xp896": -0.5}}
+
+
+def make_plan():
+    ops, hist = [], {}
+
+    def add(options, reads, writes, sem=None, inc=1, after=(), lat=0.0, behind=()):
+        n = len(ops)
+        dep = set(after)
+        for acc, is_w in ((reads, False), (writes, True)):
+            for name, lo, hi in acc:
+                for l2, h2, w2, m in hist.get(name, []):
+                    if name in BANKS or (lo < h2 and l2 < hi and (is_w or w2)):
+                        dep.add(m)
+        for name, lo, hi in writes:
+            hist[name] = [a for a in hist.get(name, []) if not (lo <= a[0] and a[1] <= hi)] + [(lo, hi, True, n)]
+        for name, lo, hi in reads:
+            hist.setdefault(name, []).append((lo, hi, False, n))
+        ops.append({"opt": options, "dep": sorted(dep), "sem": sem, "inc": inc, "lat": lat, "pe": list(options) == ["pe"],
+                    "behind": list(behind), "pri": CFG["pri"].get("%s%d" % writes[0][:2], 0.0) if writes else 0.0})
+        return n
+
+    return ops, add
+
+
+def schedule(ops):
+    n = len(ops)
+    users = [[] for _ in ops]
+    for i, o in enumerate(ops):
+        for d in o["dep"] + o["behind"]:
+            users[d].append(i)
+    tail = [0.0] * n
+    for i in range(n - 1, -1, -1):
+        own = min(c for _, c in ops[i]["opt"].values()) + ops[i]["lat"]
+        tail[i] = own + max([tail[u] + CFG["hop"] for u in users[i]] + [0.0])
+    free, done, left, order = {}, [0.0] * n, [len(o["dep"]) + len(o["behind"]) for o in ops], []
+    ready = [i for i in range(n) if left[i] == 0]
+    while ready:
+        cand = []
+        for i in ready:
+            o = ops[i]
+            t0 = max([done[d] + (0.0 if o["pe"] and ops[d]["pe"] else CFG["hop"]) for d in o["dep"]] + [0.0])
+            q = min((max(t0, free.get(q, 0.0)) + c, q) for q, (_, c) in o["opt"].items())[1]
+            cand.append((max(t0, free.get(q, 0.0)), q, i))
+        s0, q0, _ = min(cand)
+        s, q, i = max((c for c in cand if c[1] == q0 and c[0] <= s0 + CFG["delta"]), key=lambda c: (tail[c[2]] + ops[c[2]]["pri"], -c[2]))
+        free[q] = s + ops[i]["opt"][q][1]
+        done[i] = free[q] + ops[i]["lat"]
+        order.append((i, q))
+        ready.remove(i)
+        for u in users[i]:
+            left[u] -= 1
+            if left[u] == 0:
+                ready.append(u)
+    return order
+
+
+def emit(g, T, ops, order):
+    queues = {"pe": g.tensor, "ve": g.vector, "ac": g.scalar, "gp": g, "sy": g.sync}
+    clock = {q: {} for q in queues}
+    total, waited, events = {}, {}, {}
+    for i, q in order:
+        o = ops[i]
+        if q == "far":
+            total[o["sem"]] = o["inc"]
+            events[i] = (o["sem"], o["inc"], {o["sem"]: o["inc"]})
+            continue
+        best = {}
+        for d in o["dep"]:
+            ev = events[d]
+            if not (o["pe"] and ops[d]["pe"]) and (ev[0] not in best or best[ev[0]][1] < ev[1]):
+                best[ev[0]] = ev
+        for sem, val, known in sorted(best.values(), key=lambda e: -len(e[2])):
+            if clock[q].get(sem, 0) < val:
+                queues[q].wait_ge(T.sem[sem], val)
+                waited[sem] = max(waited.get(sem, 0), val)
+                for s, v in known.items():
+                    clock[q][s] = max(clock[q].get(s, 0), v)
+        ins = o["opt"][q][0](queues[q])
+        sem = o["sem"] or q
+        if ins is not None:
+            ins.then_inc(T.sem[sem], o["inc"])
+        total[sem] = total.get(sem, 0) + o["inc"]
+        known = dict(clock[q])
+        known[sem] = total[sem]
+        events[i] = (sem, total[sem], known)
+    for sem in SEMAPHORES:
+        if total.get(sem, 0) > waited.get(sem, 0):
+            g.wait_ge(T.sem[sem], total[sem])
+
+
+def rank_program(g, core, T, topo):
+    rank = T.rank_of(core)
+    if rank is None:
+        return
+    A, ACT = AluOpType, ActivationFunctionType
+    ops, add = make_plan()
+    nr = len(T.cores)
+    cyc, gam, pec = CFG["cyc"], CFG["gam"], CFG["pe"]
+    ident = T.band[:, 16:144]
+    both = ("ve", "ac")
+
+    def vec(fn, n, reads, writes):
+        return add({"ve": (fn, 0.05 + max(64, n) * cyc)}, reads, writes)
+
+    def move(qs, dst, src, cv, cs, reads, writes):
+        opt = {"ve": (lambda e: e.tensor_copy(dst, src), 0.05 + cv), "ac": (lambda e: e.activation(dst, src, ACT.Copy), 0.065 + cs)}
+        return add({q: opt[q] for q in qs}, reads, writes)
+
+    def copy(qs, dst, src, n, half, reads, writes):
+        return move(qs, dst, src, max(64, n * (0.5 if half else 1)) * cyc, max(64, n) * cyc, reads, writes)
+
+    def gather(out, lo, n, win, wn, off, olo):
+        src = T[win][:, 0:wn].indirect(T[off][:, olo // 16:(olo + n) // 16])
+        return move(both, T[out][:, lo:lo + n], src, n * gam, n * gam,
+                    [(win, 0, wn), (off, olo // 16, (olo + n) // 16)], [(out, lo, lo + n)])
+
+    def pe(calls, cycles, reads, writes):
+        def fn(e):
+            last = None
+            for c in calls:
+                last = c(e)
+            return last
+        return add({"pe": (fn, cycles * pec)}, reads, writes)
+
+    def mm(out, lhsT, rhs, start, stop):
+        return lambda e: e.matmul(out, lhsT, rhs, start, stop)
+
+    def tr(out, in_, idn):
+        return lambda e: e.transpose(out, in_, idn)
+
+    prev = {"sy": [], "ac": []}
+
+    def dma(q, dst, src, reads, writes, sem, lat=2.0, after=()):
+        prev[q].append(add({q: (lambda e: e.dma_start(dst, src), 0.1)}, reads, writes, sem, 16, after, lat, prev[q][-1:]))
+
+    cut = CFG["split"]
+    dma("sy", T.stc[:], T.st[:], [], [("stc", 0, 64)], "d_st")
+    dma("ac", T.sdr[:], T.sd[:], [], [("sdr", 0, 64)], "d_sd")
+    dma("sy", T.thr[:], T.th[:], [], [("thr", 0, 256)], "d_th", 3.0)
+    dma("ac", T.nbr[:], T.nb[:], [], [("nbr", 0, 256)], "d_nb", 3.0)
+    dma("sy", T.tbr[:], T.tb[:], [], [("tbr", 0, 256)], "d_tb", 4.0)
+    dma("sy", T.pairb[:, 0:cut], T.pair[:, 0:cut], [], [("pairb", 0, cut)], "d_p0", 8.0)
+
+    vec(lambda e: e.memset(T.ones[:], 1.0), 72, [], [("ones", 0, 144)])
+    add({"gp": (lambda e: e.affine_select(T.band[:], T.ones[:], [[-1, 144]], A.is_equal, 0.0, 16, 1), 0.5)},
+        [("ones", 0, 144)], [("band", 0, 144)])
+    add({"gp": (lambda e: e.iota(T.pat[:], [[0, 16], [1, 16]], -15, 0, allow_small_or_imprecise_dtypes=True), 0.7)},
+        [("band", 0, 144)], [("pat", 0, 256)])
+    vec(lambda e: e.memset(T.pad[:], 0.0), 384, [], [("pad", 0, 768)])
+    vec(lambda e: e.memset(T.dz[:], 0.0), 72, [], [("dz", 0, 144)])
+    vec(lambda e: e.memset(T.du[:], 0.0), 72, [], [("du", 0, 144)])
+    vec(lambda e: e.memset(T.mb[:, 0:1], 0.0), 1, [], [("mb", 0, 1)])
+    vec(lambda e: e.tensor_scalar(T.dz[:, 15:128:16], T.band[:, 31:144:16], 592.0, None, A.mult), 8, [("band", 0, 144)], [("dz", 0, 144)])
+    vec(lambda e: e.tensor_copy(T.du[:, 15:128:16], T.band[:, 31:144:16]), 8, [("band", 0, 144)], [("du", 0, 144)])
+    vec(lambda e: e.tensor_scalar(T.rst[:], T.pat[:], -15.0, BIG, A.is_equal, A.mult), 256, [("pat", 0, 256)], [("rst", 0, 256)])
+    vec(lambda e: e.tensor_copy(T.idf[:], ident), 128, [("band", 0, 144)], [("idf", 0, 128)])
+
+    vec(lambda e: e.tensor_scalar(T.stb[:], T.stc[:], -15.0, None, A.add), 64, [("stc", 0, 64)], [("stb", 0, 64)])
+    vec(lambda e: e.tensor_copy(T.sdo[:], T.sdr[:]), 64, [("sdr", 0, 64)], [("sdo", 0, 64)])
+    for part, bank in enumerate(("pa0", "pa1", "pa2", "pc")):
+        pe([mm(T[bank][:, 64 * a:64 * a + 64], T.band[:, 1 + 4 * part + a:129 + 4 * part + a], T.stb[:], True, True) for a in range(4)],
+           256, [("band", 0, 144), ("stb", 0, 64)], [(bank, 0, 256)])
+        copy(both, T.W[:, 256 * part:256 * part + 256], T[bank][:, 0:256], 256, False, [(bank, 0, 256)], [("W", 256 * part, 256 * part + 256)])
+
+    def lists(h, after):
+        for qd in range(4):
+            lo = 128 * h + 32 * qd
+            for raw, off in (("thr", "tho"), ("nbr", "nbo")):
+                add({"ve": (lambda e, raw=raw, off=off, lo=lo, qd=qd:
+                            e.tensor_copy(T[off][:, lo:lo + 32], T[raw][:, 4 * h:4 * h + 4, 8 * qd:8 * qd + 8]), 0.12)},
+                    [(raw, 0, 256)], [(off, lo, lo + 32)], after=after)
+            add({"ve": (lambda e, lo=lo, qd=qd: e.tensor_scalar(T.tbf[:, lo:lo + 32], T.tbr[:, 4 * h:4 * h + 4, 8 * qd:8 * qd + 8],
+                                                                16.0, 8895.0, A.mult, A.add), 0.12)},
+                [("tbr", 0, 256)], [("tbf", lo, lo + 32)], after=after)
+
+    def share(src, k):
+        group = [c for c in CFG["calls"] if k in c][0]
+        dst = T.cores[(T.rank_of(src) + k + 1) % nr]
+        eng = topo.engines(src, dst)
+        n = 1
+        while 2 * n * len(group) <= len(eng):
+            n *= 2
+        return eng[n * group.index(k):n * (group.index(k) + 1)]
+
+    def send(x):
+        packed, sent = [], []
+        for k, bank in enumerate(("pc", "px0", "px1")):
+            d = (rank + k + 1) % nr
+            lo = 48 * x + 16 * k
+            for e2 in range(2):
+                gather("xs", 256 * d + 128 * e2, 128, "W", 1024, "sdo", 256 * d + 128 * e2)
+            pe([mm(T[bank][:, 8 * e2:8 * e2 + 8], T.xs[:, 256 * d + 128 * e2:256 * d + 128 * e2 + 128], T.band[:, 31:144:16], True, True)
+                for e2 in range(2)], 128, [("xs", 256 * d, 256 * d + 256), ("band", 0, 144)], [(bank, 0, 16)])
+            packed.append(copy(both, T.snd[:, lo:lo + 16], T[bank][:, 0:16], 16, False, [(bank, 0, 16)], [("snd", lo, lo + 16)]))
+        for n, group in enumerate(CFG["calls"]):
+            loc = "loc%d%d" % (x, n)
+            transfers = []
+            for k in group:
+                rid, pid, _ = topo.addr(T.cores[(rank + k + 1) % nr])
+                lo = 48 * x + 16 * k
+                transfers.append(RemoteDMATransfer(dst_ids=[DstId(rid=rid, pnc=pid)], dma_engine_mask=sum(1 << c for c in share(core, k)),
+                                                   remote_sem=T.sem["arr%d%d" % (x, k)], src=T.snd[:, lo:lo + 16], dst=T.lnd[:, lo:lo + 16]))
+
+            def call(e, transfers=transfers, loc=loc):
+                e.remote_dma_fused(transfers, local_sem=T.sem[loc])
+
+            first = CFG["first"] if x == 0 and n == 0 else 0.0
+            s = add({"gp": (call, CFG["rows"] * len(group) + first)}, [("snd", 48 * x + 16 * k, 48 * x + 16 * k + 16) for k in group], [],
+                    loc, sum(len(share(core, k)) for k in group), (), CFG["lat"] / 2, sent[-1:])
+            sent.append(s)
+            for k in group:
+                lo = 48 * x + 16 * k
+                add({"far": (None, 0.0)}, [], [("lnd", lo, lo + 16)], "arr%d%d" % (x, k),
+                    len(share(T.cores[(rank - k - 1) % nr], k)), [s], CFG["lat"] / 2)
+        gather("W", 1024 + 256 * rank, 256, "W", 1024, "sdo", 256 * rank)
+        return packed, sent
+
+    def receive(x):
+        for k, bank in enumerate(("pra", "prb", "pra")):
+            lo, c = 48 * x + 16 * k, 256 * k
+            copy(both, T.pad[:, c + 15:c + 256:16], T.lnd[:, lo:lo + 16], 16, True, [("lnd", lo, lo + 16)], [("pad", c, c + 256)])
+            pe([tr(T[bank][:, c + 128 * j:c + 128 * j + 128], T.pad[:, c + 128 * j:c + 128 * j + 128], ident) for j in range(2)], 256,
+               [("pad", c, c + 256), ("band", 0, 144)], [(bank, c, c + 256)])
+            w = 1024 + 256 * ((rank - k - 1) % nr)
+            copy(both, T.W[:, w:w + 256], T[bank][:, c:c + 256], 256, True, [(bank, c, c + 256)], [("W", w, w + 256)])
+
+    def unit(u, h):
+        bank, lo = "px%d" % u, 64 * u
+        for n, (name, d) in enumerate((("th", "dz"), ("nb", "du"))):
+            s1 = CFG["s1"][2 * u + n]
+            for c in range(1024 * u, 1024 * u + 1024, s1):
+                gather("x" + name, c, s1, "W", 2048, name + "o", 2048 * h + c)
+            pe([mm(T[bank][:, 0:64], T[d][:, 15 - i:143 - i], T["x" + name][:, 1024 * u + i:1024 * u + 1024:16], n == 0 and i == 0, n == 1 and i == 15)
+                for i in range(16)], 1024, [(d, 0, 144), ("x" + name, 1024 * u, 1024 * u + 1024)], [(bank, 0, 64)])
+        vec(lambda e: e.tensor_tensor(T.ia[:, lo:lo + 64], T[bank][:, 0:64], T.tbf[:, 128 * h + lo:128 * h + lo + 64], A.add), 64,
+            [(bank, 0, 64), ("tbf", 128 * h + lo, 128 * h + lo + 64)], [("ia", lo, lo + 64)])
+        vec(lambda e: e.tensor_scalar(T.ib[:, lo:lo + 64], T.ia[:, lo:lo + 64], 8191, None, A.bitwise_and), 64,
+            [("ia", lo, lo + 64)], [("ib", lo, lo + 64)])
+        vec(lambda e: e.tensor_copy(T.po[:, lo:lo + 64], T.ib[:, lo:lo + 64]), 64, [("ib", lo, lo + 64)], [("po", lo, lo + 64)])
+
+    acc, back = {}, {}
+    for n, (q0, nq) in enumerate(CFG["low"]):
+        for k in range(nq):
+            acc[q0 + k] = (("pa0", "pa1", "pa2", "pc")[n], 128 * k)
+            back[q0 + k] = (("pra", "prb")[n % 2], 128 * (q0 + k))
+
+    def sums(qd, h):
+        bank, c = acc[qd]
+        r = 512 * h + 128 * qd
+        out = T[bank][:, c:c + 128]
+        s2 = CFG["s2"][qd]
+        for lo in range(512 * qd, 512 * qd + 512, s2):
+            gather("xp", lo, s2, "pairb", 8192, "po", lo)
+        pe([mm(out, T.ownb[:, r:r + 128], ident, True, False)], 128, [("ownb", r, r + 128), ("band", 0, 144), ("po", 32 * qd, 32 * qd + 32)],
+           [(bank, c, c + 128)])
+        for half in range(2):
+            lo = 512 * qd + 256 * half
+            pe([mm(out, T.xp[:, lo + 128 * k:lo + 128 * k + 128], ident, False, half == 1 and k == 1) for k in range(2)], 256,
+               [("xp", lo, lo + 256)], [(bank, c, c + 128)])
+
+    def lowest(q0, nq):
+        bank, c = acc[q0]
+        lo, n = 128 * q0, 128 * nq
+        vec(lambda e: e.tensor_tensor_scan(T.mb[:, lo + 1:lo + n + 1], T.rst[:, 0:n], T[bank][:, c:c + n], 0.0, A.add, A.min), n,
+            [(bank, c, c + n), ("rst", 0, 256)], [("mb", lo + 1, lo + n + 1)])
+        vec(lambda e: e.tensor_tensor(T.nd[:, lo:lo + n], T[bank][:, c:c + n], T.mb[:, lo:lo + n], A.is_ge), n,
+            [(bank, c, c + n), ("mb", lo, lo + n)], [("nd", lo, lo + n)])
+        vec(lambda e: e.tensor_tensor_scan(T.cb[:, lo:lo + n], T.nd[:, lo:lo + n], T.pat[:, 0:n], 0.0, A.mult, A.min), n // 2,
+            [("nd", lo, lo + n), ("pat", 0, 256)], [("cb", lo, lo + n)])
+
+    def renew(q0, nq, h):
+        bank, c = back[q0]
+        lo, n = 512 * h + 128 * q0, 128 * nq
+        pe([tr(T[bank][:, c + 128 * k:c + 128 * k + 128], T.cb[:, 128 * (q0 + k):128 * (q0 + k + 1)], ident) for k in range(nq)], n,
+           [("cb", 128 * q0, 128 * q0 + n)], [(bank, c, c + n)])
+        copy(both, T.W[:, lo:lo + n], T[bank][:, c:c + n], n, True, [(bank, c, c + n)], [("W", lo, lo + n)])
+
+    def results(q0, nq, h):
+        c, n = 128 * q0, 128 * nq
+        lo = 512 * h + c
+        pe([tr(T.px0[0:8, 128 * k:128 * k + 128], T.mb[:, 128 * k + 16:128 * k + 129:16], T.idf[:]) for k in range(q0, q0 + nq)], 4 * n,
+           [("mb", c + 1, c + n + 1), ("idf", 0, 128)], [("px0", c, c + n)])
+        copy(both, T.esb[0:8, lo:lo + n], T.px0[0:8, c:c + n], n, False, [("px0", c, c + n)], [("esb", lo, lo + n)])
+        pe([mm(T.px1[0:8, 128 * k:128 * k + 128], T.cb[:, 128 * k + 15:128 * k + 128:16], ident, True, True) for k in range(q0, q0 + nq)], n,
+           [("cb", c, c + n)], [("px1", c, c + n)])
+        dst, src = T.ysb[0:8, lo:lo + n], T.px1[0:8, c:c + n]
+        add({"ve": (lambda e: e.tensor_scalar(dst, src, 15.0, None, A.add), 0.05 + n * cyc),
+             "ac": (lambda e: e.activation(dst, src, ACT.Identity, bias=15.0), 0.065 + n * cyc)}, [("px1", c, c + n)], [("ysb", lo, lo + n)])
+
+    def store(h, qe):
+        lo = 512 * h
+        dma(qe, T.e[:, lo:lo + 512], T.esb[0:8, lo:lo + 512], [("esb", lo, lo + 512)], [], "d_e%d" % h)
+        dma("sy", T.y[:, lo:lo + 512], T.ysb[0:8, lo:lo + 512], [("ysb", lo, lo + 512)], [], "d_y%d" % h)
+
+    packed, sent = send(0)
+    dma("sy", T.pairb[:, cut:8192], T.pair[:, cut:8192], [], [("pairb", cut, 8192)], "d_p1", 5.5, sent[:1])
+    dma("sy", T.ownb[:], T.own[:], [], [("ownb", 0, 1024)], "d_own", 9.0)
+    lists(0, packed[-1:])
+    for t in range(ROUNDS):
+        h = t & 1
+        receive(t)
+        unit(0, h)
+        unit(1, h)
+        for q0, nq in CFG["low"]:
+            for qd in range(q0, q0 + nq):
+                sums(qd, h)
+            lowest(q0, nq)
+            if t < ROUNDS - 1:
+                renew(q0, nq, h)
+            else:
+                results(q0, nq, h)
+        if t < ROUNDS - 1:
+            packed, sent = send(t + 1)
+        if t == 0:
+            lists(1, packed[-1:])
+        if t == ROUNDS - 2:
+            results(0, 4, h)
+            store(h, "sy")
+    store((ROUNDS - 1) & 1, "ac")
+    emit(g, T, ops, schedule(ops))

@@ -2,54 +2,79 @@ from concourse.bass import DstId, RemoteDMATransfer
 from concourse.mybir import AluOpType, ActivationFunctionType
 
 BF, F32, I32, U16 = "bfloat16", "float32", "int32", "uint16"
+ROUNDS = 4
+CFG = {"gam": 1.27e-3, "cyc": 0.89e-3, "pe": 0.445e-3, "hop": 0.11, "issue": 0.2, "lat": 1.0, "row": 0.42, "first": 4.7, "delta": 0.2,
+       "wide": 1, "fused": 1, "comp": (0, 0, 0, 1, 1, 1, 2, 2), "units": ((0, 2), (2, 2)), "low": ((0, 2), (2, 1), (3, 1)), "halves": "nb3 xp1 xp2 xp3 wr2 sd0 sd1 sd2", "pri": {},
+       "again": (tuple((0, 8192 + 1024 * n, 1024) for n in range(4)) + ((0, 16384, 704),) + tuple((0, 12288 + 512 * n, 512) for n in range(8))),
+       "loads": (("th0", None, 2.2), ("nb0", None, 2.7), ("tb0", None, 3.2), ((0, 4096), None, 8.9), ((4096, 8192), "m0", 6.9),
+                 ("own0", "m0", 7.7), ("th1", "m0", 8.2), ("nb1", "m0", 8.7), ("tb1", "m0", 9.2), ("own1", "m0", 10.0)),
+       "ord": ({"ve": "ag3 ag1 ag4 th0 nb1 th2 ia0 nb2 ib0 po0 ia1 ib1 po1 xp1a xp3a xp2a mb0 nd0 mb2 cb0 mb3 nd2 nd3 cb3 cb2 "
+                      "wo3 sd0a sd1b sl0 sd2a sl1 mo ag5 sd3 pm0 wm0 wm1 ag8 wm2",
+                "ac": "ag2 ag0 th1 nb0 th3 nb3a nb3b xp1b xp0 ag7 xp2b xp3b ag9 wo0 sc0 wo2 "
+                      "sd0b sd1a sd2b sc1 sl2 pp ag11 ag6 ag12 pm1 pm2 ag10",
+                "pe": "Tth0 Tnb0 Tth1 Tnb1 So0 So2 Sa0 Sb0 So1 Sa1 So3 Sb1 Sa2 Sb2 Sa3 Sb3 "
+                      "Two0 C0 Two2 Two3 Tsl0 Tsl1 Tsl2 Tmo C1 Twm0 Twm1 Twm2 C2"},
+               {"ve": "pv0 pv1 th0 nb3b nb1 th2 po0 nb3a xp1b po1 xp2a xp3b mb0 nd0 cb0 mb2 mb3 nd2 nd3 cb2 cb3 sn3 wo co0 wr0 wr1 wr2",
+                "ac": "th1 nb0 th3 nb2 xp0 xp1a xp3a xp2b wv1 pv2 sn0 sn2 wv0 wv2 pr0 pr1 pr2 wr2s",
+                "pe": "Ttb1 Ttb0 Twv0 Twv1 Tth0 Tnb0 Tth1 So0 Tnb1 Sa0 Sb0 So1 Sa1 Sb1 So2 Sa2 So3 Sa3 Sb3 Sb2 "
+                      "C3 Two Twv2 C4 C5 Twr0 Twr1 Twr2 Twr2s"},
+               {"ve": "th0 nb1 th2 nb3a po0 nb3b xp1a po1 xp1b xp3a mb0 nd0 cb0 mb3 mb2 nd2 nd3 cb2 cb3 sn3 pr0 ys0 co1 wr0 wr1 wr2",
+                "ac": "th1 nb0 th3 nb2 xp0 xp2b xp2a xp3b sn0 sn2 wo pr1 es0 pr2 wr2s",
+                "pe": "Ttb1 Ttb0 Tth0 Tnb0 Tth1 So0 Tnb1 Sa0 Sb0 So2 So1 Sa1 Sb1 Sa2 So3 Sa3 Sb3 Sb2 "
+                      "C6 Two Te0 C7 Ty0 Twr0 Twr1 Twr2 Twr2s"},
+               {"ve": "th0 nb0 th2 nb3a po0 nb3b xp1b po1 xp2a xp3a mb0 nd0 cb0 mb2 mb3 es0 nd2 nd3 cb2 cb3 ys3",
+                "ac": "th1 nb1 th3 nb2 xp0 xp1a xp2b xp3b ys0 es2 es3 ys2",
+                "pe": "Ttb1 Ttb0 Tth0 Tnb0 Tth1 Tnb1 So0 Sa0 Sb0 So1 Sa1 Sb1 So2 So3 Sa2 Sa3 Te0 Sb2 Sb3 Ty0 Te2 Te3 Ty2 Ty3"})}
 SCRATCH = {
-    "stc": ("sbuf", [128, 64], I32), "stb": ("sbuf", [128, 64], BF),
+    "stc": ("sbuf", [128, 256], I32), "stb": ("sbuf", [128, 256], BF),
     "sdr": ("sbuf", [128, 64], I32), "sdo": ("sbuf", [128, 64], U16),
-    "thr": ("sbuf", [128, 8, 32], I32), "nbr": ("sbuf", [128, 8, 32], I32), "tbr": ("sbuf", [128, 8, 32], I32),
-    "tho": ("sbuf", [128, 256], U16), "nbo": ("sbuf", [128, 256], U16), "tbf": ("sbuf", [128, 256], F32),
-    "ownb": ("sbuf", [128, 1024], BF), "pairb": ("sbuf", [128, 8192], BF),
-    "W": ("sbuf", [128, 2048], BF),
-    "xth": ("sbuf", [128, 2048], BF), "xnb": ("sbuf", [128, 2048], BF), "xp": ("sbuf", [128, 2048], BF),
-    "xs": ("sbuf", [128, 1024], BF),
+    "raw": ("sbuf", [128, 16, 32], I32), "tbr": ("sbuf", [128, 8, 32], I32),
+    "num": ("sbuf", [128, 512], U16), "tbf": ("sbuf", [128, 256], F32),
+    "ownb": ("sbuf", [128, 1024], BF), "tab": ("sbuf", [128, 17088], BF),
+    "M": ("sbuf", [128, 2048], BF), "xs": ("sbuf", [128, 768], BF), "W": ("sbuf", [128, 4096], BF),
+    "xth": ("sbuf", [128, 6144], BF), "xnb": ("sbuf", [128, 6144], BF), "xp": ("sbuf", [128, 2048], BF),
+    "co": ("sbuf", [128, 512], U16),
     "ia": ("sbuf", [128, 128], I32), "ib": ("sbuf", [128, 128], I32), "po": ("sbuf", [128, 128], U16),
     "mb": ("sbuf", [128, 520], F32), "nd": ("sbuf", [128, 512], BF), "cb": ("sbuf", [128, 512], BF),
-    "snd": ("sbuf", [128, 192], BF), "lnd": ("sbuf", [128, 192], BF), "pad": ("sbuf", [128, 768], BF),
-    "ones": ("sbuf", [128, 144], BF), "band": ("sbuf", [128, 144], BF), "idf": ("sbuf", [128, 128], F32),
-    "dz": ("sbuf", [128, 144], BF), "du": ("sbuf", [128, 144], BF),
+    "snd0": ("sbuf", [128, 144], BF), "lnd0": ("sbuf", [128, 144], BF), "snd1": ("sbuf", [128, 112], BF),
+    "snd": ("sbuf", [128, 128], BF), "lnd": ("sbuf", [128, 336], BF),
+    "padm": ("sbuf", [128, 48, 16], BF), "padw": ("sbuf", [128, 1536], BF), "pado": ("sbuf", [128, 512], BF),
+    "D": ("sbuf", [128, 3, 144], BF), "ident": ("sbuf", [128, 128], BF), "idf": ("sbuf", [128, 128], F32),
     "pat": ("sbuf", [128, 256], BF), "rst": ("sbuf", [128, 256], F32),
+    "seln": ("sbuf", [128, 4, 8, 16], BF), "sel3": ("sbuf", [128, 24], BF),
     "ysb": ("sbuf", [128, 1024], F32), "esb": ("sbuf", [128, 1024], F32),
     "px0": ("psum", [128, 512], F32), "px1": ("psum", [128, 512], F32),
     "pa0": ("psum", [128, 512], F32), "pa1": ("psum", [128, 512], F32), "pa2": ("psum", [128, 512], F32),
-    "pc": ("psum", [128, 512], F32),
-    "pra": ("psum", [128, 1024], BF), "prb": ("psum", [128, 1024], BF),
+    "pa3": ("psum", [128, 512], F32), "pra": ("psum", [128, 1024], BF), "prb": ("psum", [128, 1024], BF),
 }
-ROUNDS = 4
-DMAS = ["d_st", "d_sd", "d_th", "d_nb", "d_tb", "d_own", "d_p0", "d_p1", "d_y0", "d_y1", "d_e0", "d_e1"]
-SEMAPHORES = ["pe", "ve", "ac", "gp"] + DMAS + ["%s%d%d" % (n, x, k) for n in ("arr", "loc") for x in range(ROUNDS) for k in range(3)]
+DMAS = ["d_st", "d_sd"] + ["d_l%d" % n for n in range(16)] + ["d_out"]
+SEMAPHORES = (["pe", "ve", "ac", "gp"] + DMAS + ["%sm%d" % (n, k) for n in ("arr", "loc") for k in range(3)]
+              + ["%s%d%d" % (n, t, k) for n in ("arr", "loc") for t in range(ROUNDS - 1) for k in range(4)])
 BANKS = [n for n in SCRATCH if SCRATCH[n][0] == "psum"]
 BIG = float(2 ** 90)
-CFG = {"gam": 1.6e-3, "cyc": 1.04e-3, "pe": 0.52e-3, "hop": 0.1, "rows": 0.7, "lat": 1.8, "first": 3.0, "delta": 0.4,
-       "s1": (512, 512, 512, 512), "s2": (256, 128, 256, 256), "calls": ((0,), (1,), (2,)), "split": 3584,
-       "low": ((0, 2), (2, 1), (3, 1)), "pri": {"ia0": 2.0, "xp1536": 0.5, "xp896": -0.5}}
+R_LO, R_HI, R_STATE = 13, 14, 15
+D_TH, D_NB, D_COL = 0, 1, 2
 
 
 def make_plan():
     ops, hist = [], {}
 
-    def add(options, reads, writes, sem=None, inc=1, after=(), lat=0.0, behind=()):
+    def add(options, reads, writes, sem=None, inc=1, after=(), lat=0.0, behind=(), name=None):
         n = len(ops)
         dep = set(after)
+        reads = [a if len(a) == 5 else tuple(a) + (0, 128) for a in reads]
+        writes = [a if len(a) == 5 else tuple(a) + (0, 128) for a in writes]
         for acc, is_w in ((reads, False), (writes, True)):
-            for name, lo, hi in acc:
-                for l2, h2, w2, m in hist.get(name, []):
-                    if name in BANKS or (lo < h2 and l2 < hi and (is_w or w2)):
+            for buf, lo, hi, p, q in acc:
+                for l2, h2, p2, q2, w2, m in hist.get(buf, []):
+                    if buf in BANKS or (lo < h2 and l2 < hi and p < q2 and p2 < q and (is_w or w2)):
                         dep.add(m)
-        for name, lo, hi in writes:
-            hist[name] = [a for a in hist.get(name, []) if not (lo <= a[0] and a[1] <= hi)] + [(lo, hi, True, n)]
-        for name, lo, hi in reads:
-            hist.setdefault(name, []).append((lo, hi, False, n))
+        for buf, lo, hi, p, q in writes:
+            hist[buf] = [a for a in hist.get(buf, []) if not (lo <= a[0] and a[1] <= hi and p <= a[2] and a[3] <= q)] + [(lo, hi, p, q, True, n)]
+        for buf, lo, hi, p, q in reads:
+            hist.setdefault(buf, []).append((lo, hi, p, q, False, n))
         ops.append({"opt": options, "dep": sorted(dep), "sem": sem, "inc": inc, "lat": lat, "pe": list(options) == ["pe"],
-                    "behind": list(behind), "pri": CFG["pri"].get("%s%d" % writes[0][:2], 0.0) if writes else 0.0})
+                    "behind": list(behind), "pri": CFG["pri"].get(name, 0.0), "name": name})
         return n
 
     return ops, add
@@ -61,8 +86,15 @@ def schedule(ops):
     for i, o in enumerate(ops):
         for d in o["dep"] + o["behind"]:
             users[d].append(i)
-    tail = [0.0] * n
-    for i in range(n - 1, -1, -1):
+    tail, left = [0.0] * n, [len(o["dep"]) + len(o["behind"]) for o in ops]
+    chain = [i for i in range(n) if left[i] == 0]
+    for i in chain:
+        for u in users[i]:
+            left[u] -= 1
+            if left[u] == 0:
+                chain.append(u)
+    assert len(chain) == n
+    for i in reversed(chain):
         own = min(c for _, c in ops[i]["opt"].values()) + ops[i]["lat"]
         tail[i] = own + max([tail[u] + CFG["hop"] for u in users[i]] + [0.0])
     free, done, left, order = {}, [0.0] * n, [len(o["dep"]) + len(o["behind"]) for o in ops], []
@@ -129,31 +161,42 @@ def rank_program(g, core, T, topo):
     ops, add = make_plan()
     nr = len(T.cores)
     cyc, gam, pec = CFG["cyc"], CFG["gam"], CFG["pe"]
-    ident = T.band[:, 16:144]
+    ident, idf = T.ident[:], T.idf[:]
     both = ("ve", "ac")
 
-    def vec(fn, n, reads, writes):
-        return add({"ve": (fn, 0.05 + max(64, n) * cyc)}, reads, writes)
+    def vec(fn, n, reads, writes, **kw):
+        return add({"ve": (fn, 0.05 + max(64, n) * cyc)}, reads, writes, **kw)
 
-    def move(qs, dst, src, cv, cs, reads, writes):
-        opt = {"ve": (lambda e: e.tensor_copy(dst, src), 0.05 + cv), "ac": (lambda e: e.activation(dst, src, ACT.Copy), 0.065 + cs)}
-        return add({q: opt[q] for q in qs}, reads, writes)
+    def pool(fn, n, reads, writes, **kw):
+        return add({"gp": (fn, 0.17 + 2 * n * cyc)}, reads, writes + [("pool", 0, 1)], **kw)
 
-    def copy(qs, dst, src, n, half, reads, writes):
-        return move(qs, dst, src, max(64, n * (0.5 if half else 1)) * cyc, max(64, n) * cyc, reads, writes)
+    def move(qs, dst, src, cv, cs, reads, writes, bias=0.0, **kw):
+        if bias:
+            opt = {"ve": (lambda e: e.tensor_scalar(dst, src, bias, None, A.add), 0.05 + cv),
+                   "ac": (lambda e: e.activation(dst, src, ACT.Identity, bias=bias), 0.065 + cs)}
+        else:
+            opt = {"ve": (lambda e: e.tensor_copy(dst, src), 0.05 + cv), "ac": (lambda e: e.activation(dst, src, ACT.Copy), 0.065 + cs)}
+        return add({q: opt[q] for q in qs}, reads, writes, **kw)
 
-    def gather(out, lo, n, win, wn, off, olo):
-        src = T[win][:, 0:wn].indirect(T[off][:, olo // 16:(olo + n) // 16])
-        return move(both, T[out][:, lo:lo + n], src, n * gam, n * gam,
-                    [(win, 0, wn), (off, olo // 16, (olo + n) // 16)], [(out, lo, lo + n)])
+    def copy(qs, dst, src, n, half, reads, writes, bias=0.0, **kw):
+        return move(qs, dst, src, max(64, n * (0.5 if half else 1)) * cyc, max(64, n) * cyc, reads, writes, bias, **kw)
 
-    def pe(calls, cycles, reads, writes):
+    def pieces(name, n):
+        return [(name + "a", 0, n // 2), (name + "b", n // 2, n // 2)] if name in CFG["halves"].split() else [(name, 0, n)]
+
+    def gather(out, lo, n, win, wn, off, olo, name=None, w=0):
+        for tag, c, m in pieces(name, n):
+            o = olo + c // 16
+            move(both, T[out][:, lo + c:lo + c + m], T[win][:, w:w + wn].indirect(T[off][:, o:o + m // 16]), m * gam, m * gam,
+                 [(win, w, w + wn), (off, o, o + m // 16)], [(out, lo + c, lo + c + m)], name=tag)
+
+    def pe(calls, cycles, reads, writes, **kw):
         def fn(e):
             last = None
             for c in calls:
                 last = c(e)
             return last
-        return add({"pe": (fn, cycles * pec)}, reads, writes)
+        return add({"pe": (fn, cycles * pec)}, reads, writes, **kw)
 
     def mm(out, lhsT, rhs, start, stop):
         return lambda e: e.matmul(out, lhsT, rhs, start, stop)
@@ -161,193 +204,306 @@ def rank_program(g, core, T, topo):
     def tr(out, in_, idn):
         return lambda e: e.transpose(out, in_, idn)
 
+    def diag(ap, n, pattern, base, value, rng):
+        return pool(lambda e: e.affine_select(ap, ap, pattern, A.not_equal, value, base, 1), n, [rng], [rng])
+
+    def iota(ap, n, pattern, base, rng, step=0):
+        return pool(lambda e: e.iota(ap, pattern, base, step, allow_small_or_imprecise_dtypes=True), n, [], [rng])
+
     prev = {"sy": [], "ac": []}
 
-    def dma(q, dst, src, reads, writes, sem, lat=2.0, after=()):
-        prev[q].append(add({q: (lambda e: e.dma_start(dst, src), 0.1)}, reads, writes, sem, 16, after, lat, prev[q][-1:]))
+    def dma(q, dst, src, reads, writes, sem, lat=1.7, after=(), in_turn=True):
+        prev[q].append(add({q: (lambda e: e.dma_start(dst, src), 0.06)}, reads, writes, sem, 16, after, lat, prev[q][-1:] if in_turn else ()))
 
-    cut = CFG["split"]
-    dma("sy", T.stc[:], T.st[:], [], [("stc", 0, 64)], "d_st")
-    dma("ac", T.sdr[:], T.sd[:], [], [("sdr", 0, 64)], "d_sd")
-    dma("sy", T.thr[:], T.th[:], [], [("thr", 0, 256)], "d_th", 3.0)
-    dma("ac", T.nbr[:], T.nb[:], [], [("nbr", 0, 256)], "d_nb", 3.0)
-    dma("sy", T.tbr[:], T.tb[:], [], [("tbr", 0, 256)], "d_tb", 4.0)
-    dma("sy", T.pairb[:, 0:cut], T.pair[:, 0:cut], [], [("pairb", 0, cut)], "d_p0", 8.0)
-
-    vec(lambda e: e.memset(T.ones[:], 1.0), 72, [], [("ones", 0, 144)])
-    add({"gp": (lambda e: e.affine_select(T.band[:], T.ones[:], [[-1, 144]], A.is_equal, 0.0, 16, 1), 0.5)},
-        [("ones", 0, 144)], [("band", 0, 144)])
-    add({"gp": (lambda e: e.iota(T.pat[:], [[0, 16], [1, 16]], -15, 0, allow_small_or_imprecise_dtypes=True), 0.7)},
-        [("band", 0, 144)], [("pat", 0, 256)])
-    vec(lambda e: e.memset(T.pad[:], 0.0), 384, [], [("pad", 0, 768)])
-    vec(lambda e: e.memset(T.dz[:], 0.0), 72, [], [("dz", 0, 144)])
-    vec(lambda e: e.memset(T.du[:], 0.0), 72, [], [("du", 0, 144)])
-    vec(lambda e: e.memset(T.mb[:, 0:1], 0.0), 1, [], [("mb", 0, 1)])
-    vec(lambda e: e.tensor_scalar(T.dz[:, 15:128:16], T.band[:, 31:144:16], 592.0, None, A.mult), 8, [("band", 0, 144)], [("dz", 0, 144)])
-    vec(lambda e: e.tensor_copy(T.du[:, 15:128:16], T.band[:, 31:144:16]), 8, [("band", 0, 144)], [("du", 0, 144)])
-    vec(lambda e: e.tensor_scalar(T.rst[:], T.pat[:], -15.0, BIG, A.is_equal, A.mult), 256, [("pat", 0, 256)], [("rst", 0, 256)])
-    vec(lambda e: e.tensor_copy(T.idf[:], ident), 128, [("band", 0, 144)], [("idf", 0, 128)])
-
-    vec(lambda e: e.tensor_scalar(T.stb[:], T.stc[:], -15.0, None, A.add), 64, [("stc", 0, 64)], [("stb", 0, 64)])
-    vec(lambda e: e.tensor_copy(T.sdo[:], T.sdr[:]), 64, [("sdr", 0, 64)], [("sdo", 0, 64)])
-    for part, bank in enumerate(("pa0", "pa1", "pa2", "pc")):
-        pe([mm(T[bank][:, 64 * a:64 * a + 64], T.band[:, 1 + 4 * part + a:129 + 4 * part + a], T.stb[:], True, True) for a in range(4)],
-           256, [("band", 0, 144), ("stb", 0, 64)], [(bank, 0, 256)])
-        copy(both, T.W[:, 256 * part:256 * part + 256], T[bank][:, 0:256], 256, False, [(bank, 0, 256)], [("W", 256 * part, 256 * part + 256)])
-
-    def lists(h, after):
-        for qd in range(4):
-            lo = 128 * h + 32 * qd
-            for raw, off in (("thr", "tho"), ("nbr", "nbo")):
-                add({"ve": (lambda e, raw=raw, off=off, lo=lo, qd=qd:
-                            e.tensor_copy(T[off][:, lo:lo + 32], T[raw][:, 4 * h:4 * h + 4, 8 * qd:8 * qd + 8]), 0.12)},
-                    [(raw, 0, 256)], [(off, lo, lo + 32)], after=after)
-            add({"ve": (lambda e, lo=lo, qd=qd: e.tensor_scalar(T.tbf[:, lo:lo + 32], T.tbr[:, 4 * h:4 * h + 4, 8 * qd:8 * qd + 8],
-                                                                16.0, 8895.0, A.mult, A.add), 0.12)},
-                [("tbr", 0, 256)], [("tbf", lo, lo + 32)], after=after)
-
-    def share(src, k):
-        group = [c for c in CFG["calls"] if k in c][0]
-        dst = T.cores[(T.rank_of(src) + k + 1) % nr]
-        eng = topo.engines(src, dst)
-        n = 1
-        while 2 * n * len(group) <= len(eng):
-            n *= 2
-        return eng[n * group.index(k):n * (group.index(k) + 1)]
-
-    def send(x):
-        packed, sent = [], []
-        for k, bank in enumerate(("pc", "px0", "px1")):
-            d = (rank + k + 1) % nr
-            lo = 48 * x + 16 * k
-            for e2 in range(2):
-                gather("xs", 256 * d + 128 * e2, 128, "W", 1024, "sdo", 256 * d + 128 * e2)
-            pe([mm(T[bank][:, 8 * e2:8 * e2 + 8], T.xs[:, 256 * d + 128 * e2:256 * d + 128 * e2 + 128], T.band[:, 31:144:16], True, True)
-                for e2 in range(2)], 128, [("xs", 256 * d, 256 * d + 256), ("band", 0, 144)], [(bank, 0, 16)])
-            packed.append(copy(both, T.snd[:, lo:lo + 16], T[bank][:, 0:16], 16, False, [(bank, 0, 16)], [("snd", lo, lo + 16)]))
-        for n, group in enumerate(CFG["calls"]):
-            loc = "loc%d%d" % (x, n)
-            transfers = []
-            for k in group:
-                rid, pid, _ = topo.addr(T.cores[(rank + k + 1) % nr])
-                lo = 48 * x + 16 * k
-                transfers.append(RemoteDMATransfer(dst_ids=[DstId(rid=rid, pnc=pid)], dma_engine_mask=sum(1 << c for c in share(core, k)),
-                                                   remote_sem=T.sem["arr%d%d" % (x, k)], src=T.snd[:, lo:lo + 16], dst=T.lnd[:, lo:lo + 16]))
-
-            def call(e, transfers=transfers, loc=loc):
-                e.remote_dma_fused(transfers, local_sem=T.sem[loc])
-
-            first = CFG["first"] if x == 0 and n == 0 else 0.0
-            s = add({"gp": (call, CFG["rows"] * len(group) + first)}, [("snd", 48 * x + 16 * k, 48 * x + 16 * k + 16) for k in group], [],
-                    loc, sum(len(share(core, k)) for k in group), (), CFG["lat"] / 2, sent[-1:])
-            sent.append(s)
-            for k in group:
-                lo = 48 * x + 16 * k
-                add({"far": (None, 0.0)}, [], [("lnd", lo, lo + 16)], "arr%d%d" % (x, k),
-                    len(share(T.cores[(rank - k - 1) % nr], k)), [s], CFG["lat"] / 2)
-        gather("W", 1024 + 256 * rank, 256, "W", 1024, "sdo", 256 * rank)
-        return packed, sent
-
-    def receive(x):
-        for k, bank in enumerate(("pra", "prb", "pra")):
-            lo, c = 48 * x + 16 * k, 256 * k
-            copy(both, T.pad[:, c + 15:c + 256:16], T.lnd[:, lo:lo + 16], 16, True, [("lnd", lo, lo + 16)], [("pad", c, c + 256)])
-            pe([tr(T[bank][:, c + 128 * j:c + 128 * j + 128], T.pad[:, c + 128 * j:c + 128 * j + 128], ident) for j in range(2)], 256,
-               [("pad", c, c + 256), ("band", 0, 144)], [(bank, c, c + 256)])
-            w = 1024 + 256 * ((rank - k - 1) % nr)
-            copy(both, T.W[:, w:w + 256], T[bank][:, c:c + 256], 256, True, [(bank, c, c + 256)], [("W", w, w + 256)])
-
-    def unit(u, h):
-        bank, lo = "px%d" % u, 64 * u
-        for n, (name, d) in enumerate((("th", "dz"), ("nb", "du"))):
-            s1 = CFG["s1"][2 * u + n]
-            for c in range(1024 * u, 1024 * u + 1024, s1):
-                gather("x" + name, c, s1, "W", 2048, name + "o", 2048 * h + c)
-            pe([mm(T[bank][:, 0:64], T[d][:, 15 - i:143 - i], T["x" + name][:, 1024 * u + i:1024 * u + 1024:16], n == 0 and i == 0, n == 1 and i == 15)
-                for i in range(16)], 1024, [(d, 0, 144), ("x" + name, 1024 * u, 1024 * u + 1024)], [(bank, 0, 64)])
-        vec(lambda e: e.tensor_tensor(T.ia[:, lo:lo + 64], T[bank][:, 0:64], T.tbf[:, 128 * h + lo:128 * h + lo + 64], A.add), 64,
-            [(bank, 0, 64), ("tbf", 128 * h + lo, 128 * h + lo + 64)], [("ia", lo, lo + 64)])
-        vec(lambda e: e.tensor_scalar(T.ib[:, lo:lo + 64], T.ia[:, lo:lo + 64], 8191, None, A.bitwise_and), 64,
-            [("ia", lo, lo + 64)], [("ib", lo, lo + 64)])
-        vec(lambda e: e.tensor_copy(T.po[:, lo:lo + 64], T.ib[:, lo:lo + 64]), 64, [("ib", lo, lo + 64)], [("po", lo, lo + 64)])
-
-    acc, back = {}, {}
-    for n, (q0, nq) in enumerate(CFG["low"]):
-        for k in range(nq):
-            acc[q0 + k] = (("pa0", "pa1", "pa2", "pc")[n], 128 * k)
-            back[q0 + k] = (("pra", "prb")[n % 2], 128 * (q0 + k))
-
-    def sums(qd, h):
-        bank, c = acc[qd]
-        r = 512 * h + 128 * qd
-        out = T[bank][:, c:c + 128]
-        s2 = CFG["s2"][qd]
-        for lo in range(512 * qd, 512 * qd + 512, s2):
-            gather("xp", lo, s2, "pairb", 8192, "po", lo)
-        pe([mm(out, T.ownb[:, r:r + 128], ident, True, False)], 128, [("ownb", r, r + 128), ("band", 0, 144), ("po", 32 * qd, 32 * qd + 32)],
-           [(bank, c, c + 128)])
-        for half in range(2):
-            lo = 512 * qd + 256 * half
-            pe([mm(out, T.xp[:, lo + 128 * k:lo + 128 * k + 128], ident, False, half == 1 and k == 1) for k in range(2)], 256,
-               [("xp", lo, lo + 256)], [(bank, c, c + 128)])
-
-    def lowest(q0, nq):
-        bank, c = acc[q0]
-        lo, n = 128 * q0, 128 * nq
-        vec(lambda e: e.tensor_tensor_scan(T.mb[:, lo + 1:lo + n + 1], T.rst[:, 0:n], T[bank][:, c:c + n], 0.0, A.add, A.min), n,
-            [(bank, c, c + n), ("rst", 0, 256)], [("mb", lo + 1, lo + n + 1)])
-        vec(lambda e: e.tensor_tensor(T.nd[:, lo:lo + n], T[bank][:, c:c + n], T.mb[:, lo:lo + n], A.is_ge), n,
-            [(bank, c, c + n), ("mb", lo, lo + n)], [("nd", lo, lo + n)])
-        vec(lambda e: e.tensor_tensor_scan(T.cb[:, lo:lo + n], T.nd[:, lo:lo + n], T.pat[:, 0:n], 0.0, A.mult, A.min), n // 2,
-            [("nd", lo, lo + n), ("pat", 0, 256)], [("cb", lo, lo + n)])
-
-    def renew(q0, nq, h):
-        bank, c = back[q0]
-        lo, n = 512 * h + 128 * q0, 128 * nq
-        pe([tr(T[bank][:, c + 128 * k:c + 128 * k + 128], T.cb[:, 128 * (q0 + k):128 * (q0 + k + 1)], ident) for k in range(nq)], n,
-           [("cb", 128 * q0, 128 * q0 + n)], [(bank, c, c + n)])
-        copy(both, T.W[:, lo:lo + n], T[bank][:, c:c + n], n, True, [(bank, c, c + n)], [("W", lo, lo + n)])
-
-    def results(q0, nq, h):
-        c, n = 128 * q0, 128 * nq
-        lo = 512 * h + c
-        pe([tr(T.px0[0:8, 128 * k:128 * k + 128], T.mb[:, 128 * k + 16:128 * k + 129:16], T.idf[:]) for k in range(q0, q0 + nq)], 4 * n,
-           [("mb", c + 1, c + n + 1), ("idf", 0, 128)], [("px0", c, c + n)])
-        copy(both, T.esb[0:8, lo:lo + n], T.px0[0:8, c:c + n], n, False, [("px0", c, c + n)], [("esb", lo, lo + n)])
-        pe([mm(T.px1[0:8, 128 * k:128 * k + 128], T.cb[:, 128 * k + 15:128 * k + 128:16], ident, True, True) for k in range(q0, q0 + nq)], n,
-           [("cb", c, c + n)], [("px1", c, c + n)])
-        dst, src = T.ysb[0:8, lo:lo + n], T.px1[0:8, c:c + n]
-        add({"ve": (lambda e: e.tensor_scalar(dst, src, 15.0, None, A.add), 0.05 + n * cyc),
-             "ac": (lambda e: e.activation(dst, src, ACT.Identity, bias=15.0), 0.065 + n * cyc)}, [("px1", c, c + n)], [("ysb", lo, lo + n)])
-
-    def store(h, qe):
-        lo = 512 * h
-        dma(qe, T.e[:, lo:lo + 512], T.esb[0:8, lo:lo + 512], [("esb", lo, lo + 512)], [], "d_e%d" % h)
-        dma("sy", T.y[:, lo:lo + 512], T.ysb[0:8, lo:lo + 512], [("ysb", lo, lo + 512)], [], "d_y%d" % h)
-
-    packed, sent = send(0)
-    dma("sy", T.pairb[:, cut:8192], T.pair[:, cut:8192], [], [("pairb", cut, 8192)], "d_p1", 5.5, sent[:1])
-    dma("sy", T.ownb[:], T.own[:], [], [("ownb", 0, 1024)], "d_own", 9.0)
-    lists(0, packed[-1:])
-    for t in range(ROUNDS):
-        h = t & 1
-        receive(t)
-        unit(0, h)
-        unit(1, h)
-        for q0, nq in CFG["low"]:
-            for qd in range(q0, q0 + nq):
-                sums(qd, h)
-            lowest(q0, nq)
-            if t < ROUNDS - 1:
-                renew(q0, nq, h)
+    def loads(gate, after):
+        for n, (name, when, lat) in enumerate(CFG["loads"]):
+            if when != gate:
+                continue
+            sem = "d_l%d" % n
+            if name in ("th0", "nb0", "th1", "nb1"):
+                h, c = int(name[2]), 8 * int(name[2]) + 4 * (name[:2] == "nb")
+                dma("sy", T.raw[:, c:c + 4, :], T[name[:2]][:, 128 * h:128 * h + 128], [], [("raw", c, c + 4)], sem, lat, after)
+                for a in range(4 if name[:2] == "nb" else 0):
+                    lo = 256 * h + 64 * a
+                    vec(lambda e, h=h, a=a, lo=lo: e.tensor_copy(T.num[:, lo:lo + 64], T.raw[:, 8 * h:8 * h + 8, 8 * a:8 * a + 8]),
+                        64, [("raw", 8 * h, 8 * h + 8)], [("num", lo, lo + 64)], name="nu%d" % a)
+            elif name in ("tb0", "tb1"):
+                h = int(name[2])
+                dma("sy", T.tbr[:, 4 * h:4 * h + 4, :], T.tb[:, 128 * h:128 * h + 128], [], [("tbr", 4 * h, 4 * h + 4)], sem, lat, after)
+                for a in range(4):
+                    c = 128 * h + 32 * a
+                    vec(lambda e, h=h, a=a, c=c: e.tensor_scalar(T.tbf[:, c:c + 32], T.tbr[:, 4 * h:4 * h + 4, 8 * a:8 * a + 8],
+                                                                 16.0, 16.0 * 593, A.mult, A.add),
+                        32, [("tbr", 4 * h, 4 * h + 4)], [("tbf", c, c + 32)], name="tb%d" % a)
+            elif name in ("own0", "own1"):
+                lo = 512 * int(name[3])
+                dma("sy", T.ownb[:, lo:lo + 512], T.own[:, lo:lo + 512], [], [("ownb", lo, lo + 512)], sem, lat, after)
             else:
-                results(q0, nq, h)
-        if t < ROUNDS - 1:
-            packed, sent = send(t + 1)
+                dma("sy", T.tab[:, name[0]:name[1]], T.pair[:, name[0]:name[1]], [], [("tab",) + name], sem, lat, after)
+
+    def remote(k, src, dst, reads, writes, name, lat, behind):
+        to = T.cores[(rank + k + 1) % nr]
+        rid, pid, _ = topo.addr(to)
+
+        def call(e):
+            e.remote_dma_fused([RemoteDMATransfer(dst_ids=[DstId(rid=rid, pnc=pid)], dma_engine_mask=topo.mask(core, to),
+                                                  remote_sem=T.sem["arr" + name], src=src, dst=dst)], local_sem=T.sem["loc" + name])
+
+        s = add({"gp": (call, CFG["issue"])}, reads, [], "loc" + name, len(topo.engines(core, to)), (), lat - 0.3, behind)
+        add({"far": (None, 0.0)}, [], writes, "arr" + name, len(topo.engines(T.cores[(rank - k - 1) % nr], core)), [s], 0.3 - CFG["hop"])
+        return s
+
+    dma("sy", T.stc[96:128, :], T.st[:], [], [("stc", 0, 256)], "d_st")
+    dma("ac", T.sdr[:], T.sd[:], [], [("sdr", 0, 64)], "d_sd")
+    loads(None, ())
+
+    vec(lambda e: e.memset(T.stb[:], 0.0), 128, [], [("stb", 0, 256)])
+    vec(lambda e: e.memset(T.seln[:], 0.0), 256, [], [("seln", 0, 512)])
+    vec(lambda e: e.memset(T.sel3[:], 0.0), 12, [], [("sel3", 0, 24)])
+    vec(lambda e: e.memset(T.stb[0:1, :], 1.0), 128, [], [("stb", 0, 256, 0, 1)])
+    iota(T.stb[64:65, :], 256, [[1, 256]], 0, ("stb", 0, 256, 64, 65))
+    diag(T.seln[96:128, :, :, R_STATE], 32, [[-1, 4], [-4, 8]], 0, 1.0, ("seln", 0, 512, 96, 128))
+    iota(T.seln[0:1, :, :, R_HI], 32, [[256, 4], [0, 8]], 1024 * rank, ("seln", 0, 512, 0, 1))
+    vec(lambda e: e.memset(T.seln[64:65, :, :, R_LO], 1.0), 16, [], [("seln", 0, 512, 64, 65)])
+    diag(T.sel3[:], 24, [[-16, 8], [-1, 3]], -R_LO, 1.0, ("sel3", 0, 24))
+    vec(lambda e: e.tensor_scalar(T.stb[96:128, :], T.stc[96:128, :], -16.0, None, A.add), 256, [("stc", 0, 256)], [("stb", 0, 256, 96, 128)])
+    vec(lambda e: e.tensor_copy(T.sdo[:], T.sdr[:]), 64, [("sdr", 0, 64)], [("sdo", 0, 64)])
+    for j in range(4):
+        bank = "pa%d" % j
+        pe([mm(T[bank][:, 0:256], T.seln[:, j, :, :], T.stb[:], True, True)], 256, [("seln", 0, 512), ("stb", 0, 256)], [(bank, 0, 256)])
+        copy(both, T.M[:, 256 * j:256 * j + 256], T[bank][:, 0:256], 256, False, [(bank, 0, 256)], [("M", 256 * j, 256 * j + 256)])
+
+    sent = []
+    for k in range(nr - 1):
+        d, bank, lo = (rank + k + 1) % nr, ("px0", "px1", "pa0")[k], 48 * k
+        for e2 in range(2):
+            gather("xs", 256 * k + 128 * e2, 128, "M", 1024, "sdo", 16 * d + 8 * e2)
+        pe([mm(T[bank][:, 24 * e2:24 * e2 + 24], T.xs[:, 256 * k + 128 * e2:256 * k + 128 * e2 + 128], T.sel3[:], True, True) for e2 in range(2)], 128,
+           [("xs", 256 * k, 256 * k + 256), ("sel3", 0, 24)], [(bank, 0, 48)])
+        packed = copy(both, T.snd0[:, lo:lo + 48], T[bank][:, 0:48], 48, False, [(bank, 0, 48)], [("snd0", lo, lo + 48)])
+        sent.append(remote(k, T.snd0[:, lo:lo + 48], T.lnd0[:, lo:lo + 48], [("snd0", lo, lo + 48)], [("lnd0", lo, lo + 48)], "m%d" % k,
+                           CFG["first"] + CFG["lat"] + 0.3 * k, sent[-1:]))
+        loads("m%d" % k, sent[-1:])
+    late = {"behind": [packed]}
+    for o in ops:
+        if o["name"]:
+            o["behind"].append(packed)
+    gather("M", 1024 + 256 * rank, 256, "M", 1024, "sdo", 16 * rank)
+    w0 = 1024 * rank
+    copy(both, T.W[:, w0 + 512:w0 + 1024], T.M[:, 512:1024], 512, True, [("M", 512, 1024)], [("W", w0 + 512, w0 + 1024)], **late)
+
+    vec(lambda e: e.memset(ident, 0.0), 64, [], [("ident", 0, 128)])
+    diag(ident, 128, [[-1, 128]], 0, 1.0, ("ident", 0, 128))
+    vec(lambda e: e.tensor_copy(idf, ident), 128, [("ident", 0, 128)], [("idf", 0, 128)], **late)
+    vec(lambda e: e.memset(T.D[:], 0.0), 216, [], [("D", 0, 3)])
+    for m, row, value in ((D_TH, R_STATE, 592.0), (D_NB, R_STATE, 1.0), (D_COL, R_LO, 1.0), (D_COL, R_HI, 1.0)):
+        diag(T.D[:, m, 15:128:16], 8, [[-16, 8]], -row, value, ("D", m, m + 1))
+    ops[iota(T.pat[:], 256, [[0, 16], [1, 16]], -16, ("pat", 0, 256))]["behind"] = sent[-1:]
+    vec(lambda e: e.tensor_scalar(T.rst[:], T.pat[:], -16.0, BIG, A.is_equal, A.mult), 256, [("pat", 0, 256)], [("rst", 0, 256)], **late)
+    vec(lambda e: e.memset(T.mb[:, 0:1], 0.0), 1, [], [("mb", 0, 1)], **late)
+    vec(lambda e: e.memset(T.padm[:], 0.0), 384, [], [("padm", 0, 3)], **late)
+    vec(lambda e: e.memset(T.padw[:], 0.0), 768, [], [("padw", 0, 3)], **late)
+    vec(lambda e: e.memset(T.pado[:], 0.0), 256, [], [("pado", 0, 4)], **late)
+    iota(T.pado[:, R_LO:512:16], 32, [[0, 2], [128, 2], [0, 8]], 0, ("pado", 0, 4), 1)
+    iota(T.pado[:, R_HI:512:16], 32, [[256, 2], [0, 2], [0, 8]], 1024 * rank, ("pado", 0, 4))
+
+    def spread(k, src, rng, h, tag):
+        w, name = 1024 * ((rank - k - 1) % nr) + 512 * h, "w%s%d" % (tag, k)
+        copy(both, T.padw[:, 512 * k + 15:512 * k + 512:16], src, 32, True, [rng], [("padw", k, k + 1)], name="p%s%d" % (tag, k))
+        m = 384 if name in CFG["halves"].split() else 512
+        bank, c = ("pra", "prb")[k & 1], 512 * (k // 2)
+        if m < 512:
+            pe([mm(T.pa2[:, 0:128], T.padw[:, 512 * k + 384:512 * k + 512], ident, True, True)], 128,
+               [("padw", k, k + 1), ("ident", 0, 128)], [("pa2", 0, 128)], name="T" + name + "s")
+            copy(both, T.W[:, w + m:w + 512], T.pa2[:, 0:128], 128, False, [("pa2", 0, 128)], [("W", w + m, w + 512)], name=name + "s")
+        pe([tr(T[bank][:, c + j:c + j + 128], T.padw[:, 512 * k + j:512 * k + j + 128], ident) for j in range(0, m, 128)], m,
+           [("padw", k, k + 1), ("ident", 0, 128)], [(bank, c, c + m)], name="T" + name)
+        copy(both, T.W[:, w:w + m], T[bank][:, c:c + m], m, True, [(bank, c, c + m)], [("W", w, w + m)], name=name)
+
+    def listed(k, row, src, rng):
+        bank, c = ("pra", "prb")[k & 1], 512 * (k // 2)
+        w = 1024 + 256 * ((rank - k - 1) % nr)
+        copy(both, T.padm[:, 16 * k:16 * k + 16, row:16], src, 48, True, [rng], [("padm", k, k + 1)], name="pm%d" % k)
+        pe([tr(T[bank][:, c + 128 * j:c + 128 * j + 128], T.padm[:, 16 * k + 8 * j:16 * k + 8 * j + 8, :], ident) for j in range(2)], 256,
+           [("padm", k, k + 1), ("ident", 0, 128)], [(bank, c, c + 256)], name="Twm%d" % k)
+        copy(both, T.M[:, w:w + 256], T[bank][:, c:c + 256], 256, True, [(bank, c, c + 256)], [("M", w, w + 256)], name="wm%d" % k)
+
+    for k in range(nr - 1):
+        listed(k, R_LO, T.lnd0[:, 48 * k:48 * k + 48], ("lnd0", 48 * k, 48 * k + 48))
+
+    def turn(bank, col, m, x, lo, n, start, stop, **kw):
+        return pe([mm(T[bank][:, col:col + n // 16], T.D[:, m, 15 - i:143 - i], T[x][:, lo + i:lo + n:16], start and i == 0, stop and i == 15)
+                   for i in range(16)], max(1024, n), [("D", m, m + 1), (x, lo, lo + n)], [(bank, col, col + n // 16)], **kw)
+
+    def compose(n):
+        h, c = n // 4, 64 * n
+        turn("pa3", c, D_COL, ("xth", "xnb")[n // 2 & 1], 2048 * h + 1024 * (n & 1), 1024, True, True, name="C%d" % n)
+        if n & 3 == 3:
+            vec(lambda e: e.tensor_copy(T.co[:, 256 * h:256 * h + 256], T.pa3[:, 256 * h:256 * h + 256]), 256,
+                [("pa3", 256 * h, 256 * h + 256)], [("co", 256 * h, 256 * h + 256)], name="co%d" % h)
+
+    def offsets(u, a0, na, t):
+        h, lo, n, bank = t & 1, 32 * a0, 32 * na, "px%d" % (u & 1)
+        x0 = 2048 * min(t, 2)
+        for k, x in enumerate(("th", "nb")):
+            for a in range(a0, a0 + na):
+                if t < 2:
+                    gather("x" + x, x0 + 512 * a, 512, "M", 2048, "num", 256 * h + 64 * a + 32 * k, "%s%d" % (x, a))
+                else:
+                    gather("x" + x, x0 + 512 * a, 512, "W", 4096, "co", 256 * h + 128 * k + 32 * a, "%s%d" % (x, a))
+            if k == 0 and t >= CFG["wide"]:
+                pe([mm(T[bank][:, 0:n], idf, T.tbf[:, 128 * h + lo:128 * h + lo + n], True, False)], 256,
+                   [("idf", 0, 128), ("tbf", 128 * h + lo, 128 * h + lo + n)], [(bank, 0, n)], name="Ttb%d" % u)
+            turn(bank, 0, (D_TH, D_NB)[k], "x" + x, x0 + 512 * a0, 512 * na, k == 0 and t < CFG["wide"], k == 1, name="T%s%d" % (x, u))
+        if t >= CFG["wide"]:
+            vec(lambda e: e.tensor_copy(T.po[:, lo:lo + n], T[bank][:, 0:n]), n, [(bank, 0, n)], [("po", lo, lo + n)], name="po%d" % u)
+            return
+        vec(lambda e: e.tensor_tensor(T.ia[:, lo:lo + n], T[bank][:, 0:n], T.tbf[:, 128 * h + lo:128 * h + lo + n], A.add), n,
+            [(bank, 0, n), ("tbf", 128 * h + lo, 128 * h + lo + n)], [("ia", lo, lo + n)], name="ia%d" % u)
+        vec(lambda e: e.tensor_scalar(T.ib[:, lo:lo + n], T.ia[:, lo:lo + n], 8191, None, A.bitwise_and), n,
+            [("ia", lo, lo + n)], [("ib", lo, lo + n)], name="ib%d" % u)
+        vec(lambda e: e.tensor_copy(T.po[:, lo:lo + n], T.ib[:, lo:lo + n]), n, [("ib", lo, lo + n)], [("po", lo, lo + n)], name="po%d" % u)
+
+    acc = {}
+    for n, (a0, na) in enumerate(CFG["low"]):
+        for k in range(na):
+            acc[a0 + k] = ("pa%d" % n, 128 * k)
+
+    def sums(a, t):
+        bank, c = acc[a]
+        r = 512 * (t & 1) + 128 * a
+        out = T[bank][:, c:c + 128]
+        gather("xp", 512 * a, 512, "tab", 17088 if t >= CFG["wide"] else 8192, "po", 32 * a, "xp%d" % a)
+        pe([mm(out, T.ownb[:, r:r + 128], ident, True, False)], 128, [("ownb", r, r + 128), ("ident", 0, 128), ("po", 32 * a, 32 * a + 32)],
+           [(bank, c, c + 128)], name="So%d" % a)
+        for half in range(2):
+            lo = 512 * a + 256 * half
+            pe([mm(out, T.xp[:, lo + 128 * k:lo + 128 * k + 128], ident, False, half == 1 and k == 1) for k in range(2)], 256,
+               [("xp", lo, lo + 256)], [(bank, c, c + 128)], name="S%s%d" % ("ab"[half], a))
+
+    def lowest(a0, na, t):
+        bank, c = acc[a0]
+        lo, n = 128 * a0, 128 * na
+        vec(lambda e: e.tensor_tensor_scan(T.mb[:, lo + 1:lo + n + 1], T.rst[:, 0:n], T[bank][:, c:c + n], 0.0, A.add, A.min), n,
+            [(bank, c, c + n), ("rst", 0, 256)], [("mb", lo + 1, lo + n + 1)], name="mb%d" % a0)
+        vec(lambda e: e.tensor_tensor(T.nd[:, lo:lo + n], T[bank][:, c:c + n], T.mb[:, lo:lo + n], A.is_ge), n,
+            [(bank, c, c + n), ("mb", lo, lo + n)], [("nd", lo, lo + n)], name="nd%d" % a0)
+        vec(lambda e: e.tensor_tensor_scan(T.cb[:, lo:lo + n], T.nd[:, lo:lo + n], T.pat[:, 0:n], 0.0, A.mult, A.min), n // 2,
+            [("nd", lo, lo + n), ("pat", 0, 256)], [("cb", lo, lo + n)], name="cb%d" % a0)
+        if 0 < t < ROUNDS - 1:
+            s0 = 32 * t + 8 * a0
+            copy(both, T.snd[:, s0:s0 + 8 * na], T.cb[:, lo + 15:lo + n:16], 8 * na, True, [("cb", lo, lo + n)], [("snd", s0, s0 + 8 * na)], name="sn%d" % a0)
         if t == 0:
-            lists(1, packed[-1:])
+            back = ("pra", "prb")[a0 & 1]
+            pe([tr(T[back][:, 128 * a:128 * a + 128], T.cb[:, 128 * a:128 * a + 128], ident) for a in range(a0, a0 + na)], n,
+               [("cb", lo, lo + n), ("ident", 0, 128)], [(back, lo, lo + n)], name="Two%d" % a0)
+            copy(both, T.W[:, w0 + lo:w0 + lo + n], T[back][:, lo:lo + n], n, True, [(back, lo, lo + n)], [("W", w0 + lo, w0 + lo + n)], name="wo%d" % a0)
+
+    def share_listed():
+        sent = []
+        for n, c in enumerate((16, 80)):
+            copy(both, T.snd1[:, c:c + 32], T.cb[:, 15:512:16], 32, True, [("cb", 0, 512)], [("snd1", c, c + 32)], name="sc%d" % n)
+        for k, (lo, c) in enumerate(((0, 0), (16, 48), (64, 64))):
+            d, bank = (rank + k + 1) % nr, ("px0", "px1", "pa2")[k]
+            gather("xs", 256 * k, 256, "W", 1024, "sdo", 16 * d, "sd%d" % k, w0)
+            pe([mm(T[bank][:, 8 * e2:8 * e2 + 8], T.xs[:, 256 * k + 128 * e2:256 * k + 128 * e2 + 128], T.ident[:, 15:128:16], True, True) for e2 in range(2)],
+               128, [("xs", 256 * k, 256 * k + 256), ("ident", 0, 128)], [(bank, 0, 16)], name="Tsl%d" % k)
+            copy(both, T.snd1[:, c:c + 16], T[bank][:, 0:16], 16, False, [(bank, 0, 16)], [("snd1", c, c + 16)], name="sl%d" % k)
+            sent.append(remote(k, T.snd1[:, lo:lo + 48], T.lnd[:, 48 * k:48 * k + 48], [("snd1", lo, lo + 48)], [("lnd", 48 * k, 48 * k + 48)],
+                               "0%d" % k, CFG["lat"] + CFG["row"], sent[-1:]))
+        loads("x0", sent[-1:])
+        copy(both, T.pado[:, 15:512:16], T.cb[:, 15:512:16], 32, True, [("cb", 0, 512)], [("pado", 0, 4)], name="pp")
+        pe([tr(T.prb[:, 512 + 128 * a:640 + 128 * a], T.pado[:, 128 * a:128 * a + 128], ident) for a in range(4)], 512,
+           [("pado", 0, 4), ("ident", 0, 128)], [("prb", 512, 1024)], name="Tmo")
+        copy(both, T.M[:, 0:512], T.prb[:, 512:1024], 512, True, [("prb", 512, 1024)], [("M", 0, 512)], name="mo")
+        gather("M", 1024 + 256 * rank, 256, "M", 1024, "sdo", 16 * rank, "sd3")
+        for k in range(nr - 1):
+            c = 48 * k + (0, 32, 0)[k]
+            listed(k, R_STATE, T.lnd[:, c:c + 16], ("lnd", 48 * k, 48 * k + 48))
+
+    def catch_up():
+        for k in range(nr - 1):
+            c = 48 * k + (16, 0, 16)[k]
+            spread(k, T.lnd[:, c:c + 32], ("lnd", 48 * k, 48 * k + 48), 0, "v")
+
+    def share(t):
+        h, sent = t & 1, []
+        if CFG["fused"]:
+            to = [T.cores[(rank + k + 1) % nr] for k in range(nr - 1)]
+            mask = topo.mask(core, to[0]) & topo.mask(core, to[1]) & topo.mask(core, to[2])
+            n = bin(mask).count("1")
+
+            def call(e):
+                e.remote_dma_fused([RemoteDMATransfer(dst_ids=[DstId(rid=topo.addr(c)[0], pnc=topo.addr(c)[1]) for c in to], dma_engine_mask=mask,
+                                                      remote_sem=T.sem["arr%d%d" % (t, rank)], src=T.snd[:, 32 * t:32 * t + 32],
+                                                      dsts=[T.lnd[:, 96 * t + 32 * k + 48:96 * t + 32 * k + 80] for k in range(nr - 1)])],
+                                   local_sem=T.sem["loc%d0" % t])
+
+            s = add({"gp": (call, CFG["issue"])}, [("snd", 32 * t, 32 * t + 32)], [], "loc%d0" % t, n, (), CFG["lat"])
+            for k in range(nr - 1):
+                lo = 96 * t + 32 * k + 48
+                add({"far": (None, 0.0)}, [], [("lnd", lo, lo + 32)], "arr%d%d" % (t, (rank - k - 1) % nr), n, [s], CFG["row"] * (k + 1) - CFG["hop"])
+        for k in range(0 if CFG["fused"] else nr - 1):
+            lo = 96 * t + 32 * k + 48
+            sent.append(remote(k, T.snd[:, 32 * t:32 * t + 32], T.lnd[:, lo:lo + 32], [("snd", 32 * t, 32 * t + 32)], [("lnd", lo, lo + 32)],
+                               "%d%d" % (t, k), CFG["lat"] + CFG["row"] + (CFG["row"] - CFG["issue"]) * k, sent[-1:]))
+        w = 1024 * rank + 512 * h
+        pe([tr(T.prb[:, 512 + 128 * a:640 + 128 * a], T.cb[:, 128 * a:128 * a + 128], ident) for a in range(4)], 512,
+           [("cb", 0, 512), ("ident", 0, 128)], [("prb", 512, 1024)], name="Two")
+        copy(both, T.W[:, w:w + 512], T.prb[:, 512:1024], 512, True, [("prb", 512, 1024)], [("W", w, w + 512)], name="wo")
+        for k in range(nr - 1):
+            lo = 96 * t + 32 * k + 48
+            spread(k, T.lnd[:, lo:lo + 32], ("lnd", lo, lo + 32), h, "r")
+
+    def store(a0, na, h, banks):
+        lo, n, c = 128 * a0, 128 * na, 512 * h + 128 * a0
+        for out, buf, bank, bias in ((T.e, "esb", banks[0], 0.0), (T.y, "ysb", banks[1], 16.0)):
+            if bias:
+                pe([mm(T[bank][0:8 * na, 0:128], T.cb[:, lo + 15:lo + n:16], ident, True, True)], 128,
+                   [("cb", lo, lo + n), ("ident", 0, 128)], [(bank, 0, 128)], name="Ty%d" % a0)
+            else:
+                pe([tr(T[bank][0:8 * na, 0:128], T.mb[:, lo + 16:lo + n + 1:16], idf)], 512,
+                   [("mb", lo + 1, lo + n + 1), ("idf", 0, 128)], [(bank, 0, 128)], name="Te%d" % a0)
+            copy(both, T[buf][0:8 * na, c:c + 128], T[bank][0:8 * na, 0:128], 128, False, [(bank, 0, 128)], [(buf, c, c + 128)], bias,
+                 name="%s%d" % (buf[:2], a0))
+            for a in range(na):
+                dma("ac" if bias and a0 == 3 else "sy", out[:, c + 128 * a:c + 128 * a + 128], T[buf][8 * a:8 * a + 8, c:c + 128],
+                    [(buf, c, c + 128)], [], "d_out", 1.5, (), False)
+
+    def arrange(start, order):
+        named = {o["name"]: n for n, o in enumerate(ops) if n >= start}
+        for q, names in order.items():
+            line = [named[x] for x in names.split() if x in named]
+            for a, b in zip([None] + line, line):
+                ops[b]["opt"] = {q: ops[b]["opt"][q]}
+                ops[b]["behind"] += [a] if a is not None else []
+
+    for t in range(ROUNDS):
+        start = len(ops)
+        for u, (a0, na) in enumerate(CFG["units"] if t else ((0, 2), (2, 2))):
+            offsets(u, a0, na, t)
+        for n, when in enumerate(CFG["comp"]):
+            if when == t:
+                compose(n)
+        for n, (when, lo, m) in enumerate(CFG["again"]):
+            if when == t:
+                copy(both, T.tab[:, lo:lo + m], T.tab[:, lo % 8192:lo % 8192 + m], m, True, [("tab", lo % 8192, lo % 8192 + m)], [("tab", lo, lo + m)],
+                     name="ag%d" % n)
+        for a0, na in CFG["low"]:
+            for a in range(a0, a0 + na):
+                sums(a, t)
+            lowest(a0, na, t)
+            if t == ROUNDS - 1:
+                store(a0, na, 1, (("px0", "px1"), None, ("pa3", "px0"), ("px1", "pa0"))[a0])
+        if t == 0:
+            share_listed()
+        if t == 1:
+            catch_up()
+        if 0 < t < ROUNDS - 1:
+            share(t)
         if t == ROUNDS - 2:
-            results(0, 4, h)
-            store(h, "sy")
-    store((ROUNDS - 1) & 1, "ac")
+            store(0, 4, 0, ("pa0", "pa1"))
+        arrange(start, CFG["ord"][t])
+        for o in ops[start:]:
+            o["seg"] = t
     emit(g, T, ops, schedule(ops))

from concourse.bass import DstId, RemoteDMATransfer
from concourse.mybir import AluOpType, ActivationFunctionType

BF, F32, I32, U16 = "bfloat16", "float32", "int32", "uint16"
ROUNDS = 4
CFG = {"gam": 1.27e-3, "cyc": 0.89e-3, "pe": 0.445e-3, "hop": 0.11, "issue": 0.2, "lat": 1.0, "row": 0.42, "first": 4.7, "delta": 0.2,
       "wide": 1, "fused": 1, "comp": (0, 0, 0, 1, 1, 1, 2, 2), "units": ((0, 2), (2, 2)), "low": ((0, 2), (2, 1), (3, 1)), "halves": "nb3 xp1 xp2 xp3 wr2 sd0 sd1 sd2", "pri": {},
       "again": (tuple((0, 8192 + 1024 * n, 1024) for n in range(4)) + ((0, 16384, 704),) + tuple((0, 12288 + 512 * n, 512) for n in range(8))),
       "loads": (("th0", None, 2.2), ("nb0", None, 2.7), ("tb0", None, 3.2), ((0, 4096), None, 8.9), ((4096, 8192), "m0", 6.9),
                 ("own0", "m0", 7.7), ("th1", "m0", 8.2), ("nb1", "m0", 8.7), ("tb1", "m0", 9.2), ("own1", "m0", 10.0)),
       "ord": ({"ve": "ag3 ag1 ag4 th0 nb1 th2 ia0 nb2 ib0 po0 ia1 ib1 po1 xp1a xp3a xp2a mb0 nd0 mb2 cb0 mb3 nd2 nd3 cb3 cb2 "
                      "wo3 sd0a sd1b sl0 sd2a sl1 mo ag5 sd3 pm0 wm0 wm1 ag8 wm2",
                "ac": "ag2 ag0 th1 nb0 th3 nb3a nb3b xp1b xp0 ag7 xp2b xp3b ag9 wo0 sc0 wo2 "
                      "sd0b sd1a sd2b sc1 sl2 pp ag11 ag6 ag12 pm1 pm2 ag10",
                "pe": "Tth0 Tnb0 Tth1 Tnb1 So0 So2 Sa0 Sb0 So1 Sa1 So3 Sb1 Sa2 Sb2 Sa3 Sb3 "
                      "Two0 C0 Two2 Two3 Tsl0 Tsl1 Tsl2 Tmo C1 Twm0 Twm1 Twm2 C2"},
               {"ve": "pv0 pv1 th0 nb3b nb1 th2 po0 nb3a xp1b po1 xp2a xp3b mb0 nd0 cb0 mb2 mb3 nd2 nd3 cb2 cb3 sn3 wo co0 wr0 wr1 wr2",
                "ac": "th1 nb0 th3 nb2 xp0 xp1a xp3a xp2b wv1 pv2 sn0 sn2 wv0 wv2 pr0 pr1 pr2 wr2s",
                "pe": "Ttb1 Ttb0 Twv0 Twv1 Tth0 Tnb0 Tth1 So0 Tnb1 Sa0 Sb0 So1 Sa1 Sb1 So2 Sa2 So3 Sa3 Sb3 Sb2 "
                      "C3 Two Twv2 C4 C5 Twr0 Twr1 Twr2 Twr2s"},
               {"ve": "th0 nb1 th2 nb3a po0 nb3b xp1a po1 xp1b xp3a mb0 nd0 cb0 mb3 mb2 nd2 nd3 cb2 cb3 sn3 pr0 ys0 co1 wr0 wr1 wr2",
                "ac": "th1 nb0 th3 nb2 xp0 xp2b xp2a xp3b sn0 sn2 wo pr1 es0 pr2 wr2s",
                "pe": "Ttb1 Ttb0 Tth0 Tnb0 Tth1 So0 Tnb1 Sa0 Sb0 So2 So1 Sa1 Sb1 Sa2 So3 Sa3 Sb3 Sb2 "
                      "C6 Two Te0 C7 Ty0 Twr0 Twr1 Twr2 Twr2s"},
               {"ve": "th0 nb0 th2 nb3a po0 nb3b xp1b po1 xp2a xp3a mb0 nd0 cb0 mb2 mb3 es0 nd2 nd3 cb2 cb3 ys3",
                "ac": "th1 nb1 th3 nb2 xp0 xp1a xp2b xp3b ys0 es2 es3 ys2",
                "pe": "Ttb1 Ttb0 Tth0 Tnb0 Tth1 Tnb1 So0 Sa0 Sb0 So1 Sa1 Sb1 So2 So3 Sa2 Sa3 Te0 Sb2 Sb3 Ty0 Te2 Te3 Ty2 Ty3"})}
SCRATCH = {
    "stc": ("sbuf", [128, 256], I32), "stb": ("sbuf", [128, 256], BF),
    "sdr": ("sbuf", [128, 64], I32), "sdo": ("sbuf", [128, 64], U16),
    "raw": ("sbuf", [128, 16, 32], I32), "tbr": ("sbuf", [128, 8, 32], I32),
    "num": ("sbuf", [128, 512], U16), "tbf": ("sbuf", [128, 256], F32),
    "ownb": ("sbuf", [128, 1024], BF), "tab": ("sbuf", [128, 17088], BF),
    "M": ("sbuf", [128, 2048], BF), "xs": ("sbuf", [128, 768], BF), "W": ("sbuf", [128, 4096], BF),
    "xth": ("sbuf", [128, 6144], BF), "xnb": ("sbuf", [128, 6144], BF), "xp": ("sbuf", [128, 2048], BF),
    "co": ("sbuf", [128, 512], U16),
    "ia": ("sbuf", [128, 128], I32), "ib": ("sbuf", [128, 128], I32), "po": ("sbuf", [128, 128], U16),
    "mb": ("sbuf", [128, 520], F32), "nd": ("sbuf", [128, 512], BF), "cb": ("sbuf", [128, 512], BF),
    "snd0": ("sbuf", [128, 144], BF), "lnd0": ("sbuf", [128, 144], BF), "snd1": ("sbuf", [128, 112], BF),
    "snd": ("sbuf", [128, 128], BF), "lnd": ("sbuf", [128, 336], BF),
    "padm": ("sbuf", [128, 48, 16], BF), "padw": ("sbuf", [128, 1536], BF), "pado": ("sbuf", [128, 512], BF),
    "D": ("sbuf", [128, 3, 144], BF), "ident": ("sbuf", [128, 128], BF), "idf": ("sbuf", [128, 128], F32),
    "pat": ("sbuf", [128, 256], BF), "rst": ("sbuf", [128, 256], F32),
    "seln": ("sbuf", [128, 4, 8, 16], BF), "sel3": ("sbuf", [128, 24], BF),
    "ysb": ("sbuf", [128, 1024], F32), "esb": ("sbuf", [128, 1024], F32),
    "px0": ("psum", [128, 512], F32), "px1": ("psum", [128, 512], F32),
    "pa0": ("psum", [128, 512], F32), "pa1": ("psum", [128, 512], F32), "pa2": ("psum", [128, 512], F32),
    "pa3": ("psum", [128, 512], F32), "pra": ("psum", [128, 1024], BF), "prb": ("psum", [128, 1024], BF),
}
DMAS = ["d_st", "d_sd"] + ["d_l%d" % n for n in range(16)] + ["d_out"]
SEMAPHORES = (["pe", "ve", "ac", "gp"] + DMAS + ["%sm%d" % (n, k) for n in ("arr", "loc") for k in range(3)]
              + ["%s%d%d" % (n, t, k) for n in ("arr", "loc") for t in range(ROUNDS - 1) for k in range(4)])
BANKS = [n for n in SCRATCH if SCRATCH[n][0] == "psum"]
BIG = float(2 ** 90)
R_LO, R_HI, R_STATE = 13, 14, 15
D_TH, D_NB, D_COL = 0, 1, 2


def make_plan():
    ops, hist = [], {}

    def add(options, reads, writes, sem=None, inc=1, after=(), lat=0.0, behind=(), name=None):
        n = len(ops)
        dep = set(after)
        reads = [a if len(a) == 5 else tuple(a) + (0, 128) for a in reads]
        writes = [a if len(a) == 5 else tuple(a) + (0, 128) for a in writes]
        for acc, is_w in ((reads, False), (writes, True)):
            for buf, lo, hi, p, q in acc:
                for l2, h2, p2, q2, w2, m in hist.get(buf, []):
                    if buf in BANKS or (lo < h2 and l2 < hi and p < q2 and p2 < q and (is_w or w2)):
                        dep.add(m)
        for buf, lo, hi, p, q in writes:
            hist[buf] = [a for a in hist.get(buf, []) if not (lo <= a[0] and a[1] <= hi and p <= a[2] and a[3] <= q)] + [(lo, hi, p, q, True, n)]
        for buf, lo, hi, p, q in reads:
            hist.setdefault(buf, []).append((lo, hi, p, q, False, n))
        ops.append({"opt": options, "dep": sorted(dep), "sem": sem, "inc": inc, "lat": lat, "pe": list(options) == ["pe"],
                    "behind": list(behind), "pri": CFG["pri"].get(name, 0.0), "name": name})
        return n

    return ops, add


def schedule(ops):
    n = len(ops)
    users = [[] for _ in ops]
    for i, o in enumerate(ops):
        for d in o["dep"] + o["behind"]:
            users[d].append(i)
    tail, left = [0.0] * n, [len(o["dep"]) + len(o["behind"]) for o in ops]
    chain = [i for i in range(n) if left[i] == 0]
    for i in chain:
        for u in users[i]:
            left[u] -= 1
            if left[u] == 0:
                chain.append(u)
    assert len(chain) == n
    for i in reversed(chain):
        own = min(c for _, c in ops[i]["opt"].values()) + ops[i]["lat"]
        tail[i] = own + max([tail[u] + CFG["hop"] for u in users[i]] + [0.0])
    free, done, left, order = {}, [0.0] * n, [len(o["dep"]) + len(o["behind"]) for o in ops], []
    ready = [i for i in range(n) if left[i] == 0]
    while ready:
        cand = []
        for i in ready:
            o = ops[i]
            t0 = max([done[d] + (0.0 if o["pe"] and ops[d]["pe"] else CFG["hop"]) for d in o["dep"]] + [0.0])
            q = min((max(t0, free.get(q, 0.0)) + c, q) for q, (_, c) in o["opt"].items())[1]
            cand.append((max(t0, free.get(q, 0.0)), q, i))
        s0, q0, _ = min(cand)
        s, q, i = max((c for c in cand if c[1] == q0 and c[0] <= s0 + CFG["delta"]), key=lambda c: (tail[c[2]] + ops[c[2]]["pri"], -c[2]))
        free[q] = s + ops[i]["opt"][q][1]
        done[i] = free[q] + ops[i]["lat"]
        order.append((i, q))
        ready.remove(i)
        for u in users[i]:
            left[u] -= 1
            if left[u] == 0:
                ready.append(u)
    return order


def emit(g, T, ops, order):
    queues = {"pe": g.tensor, "ve": g.vector, "ac": g.scalar, "gp": g, "sy": g.sync}
    clock = {q: {} for q in queues}
    total, waited, events = {}, {}, {}
    for i, q in order:
        o = ops[i]
        if q == "far":
            total[o["sem"]] = o["inc"]
            events[i] = (o["sem"], o["inc"], {o["sem"]: o["inc"]})
            continue
        best = {}
        for d in o["dep"]:
            ev = events[d]
            if not (o["pe"] and ops[d]["pe"]) and (ev[0] not in best or best[ev[0]][1] < ev[1]):
                best[ev[0]] = ev
        for sem, val, known in sorted(best.values(), key=lambda e: -len(e[2])):
            if clock[q].get(sem, 0) < val:
                queues[q].wait_ge(T.sem[sem], val)
                waited[sem] = max(waited.get(sem, 0), val)
                for s, v in known.items():
                    clock[q][s] = max(clock[q].get(s, 0), v)
        ins = o["opt"][q][0](queues[q])
        sem = o["sem"] or q
        if ins is not None:
            ins.then_inc(T.sem[sem], o["inc"])
        total[sem] = total.get(sem, 0) + o["inc"]
        known = dict(clock[q])
        known[sem] = total[sem]
        events[i] = (sem, total[sem], known)
    for sem in SEMAPHORES:
        if total.get(sem, 0) > waited.get(sem, 0):
            g.wait_ge(T.sem[sem], total[sem])


def rank_program(g, core, T, topo):
    rank = T.rank_of(core)
    if rank is None:
        return
    A, ACT = AluOpType, ActivationFunctionType
    ops, add = make_plan()
    nr = len(T.cores)
    cyc, gam, pec = CFG["cyc"], CFG["gam"], CFG["pe"]
    ident, idf = T.ident[:], T.idf[:]
    both = ("ve", "ac")

    def vec(fn, n, reads, writes, **kw):
        return add({"ve": (fn, 0.05 + max(64, n) * cyc)}, reads, writes, **kw)

    def pool(fn, n, reads, writes, **kw):
        return add({"gp": (fn, 0.17 + 2 * n * cyc)}, reads, writes + [("pool", 0, 1)], **kw)

    def move(qs, dst, src, cv, cs, reads, writes, bias=0.0, **kw):
        if bias:
            opt = {"ve": (lambda e: e.tensor_scalar(dst, src, bias, None, A.add), 0.05 + cv),
                   "ac": (lambda e: e.activation(dst, src, ACT.Identity, bias=bias), 0.065 + cs)}
        else:
            opt = {"ve": (lambda e: e.tensor_copy(dst, src), 0.05 + cv), "ac": (lambda e: e.activation(dst, src, ACT.Copy), 0.065 + cs)}
        return add({q: opt[q] for q in qs}, reads, writes, **kw)

    def copy(qs, dst, src, n, half, reads, writes, bias=0.0, **kw):
        return move(qs, dst, src, max(64, n * (0.5 if half else 1)) * cyc, max(64, n) * cyc, reads, writes, bias, **kw)

    def pieces(name, n):
        return [(name + "a", 0, n // 2), (name + "b", n // 2, n // 2)] if name in CFG["halves"].split() else [(name, 0, n)]

    def gather(out, lo, n, win, wn, off, olo, name=None, w=0):
        for tag, c, m in pieces(name, n):
            o = olo + c // 16
            move(both, T[out][:, lo + c:lo + c + m], T[win][:, w:w + wn].indirect(T[off][:, o:o + m // 16]), m * gam, m * gam,
                 [(win, w, w + wn), (off, o, o + m // 16)], [(out, lo + c, lo + c + m)], name=tag)

    def pe(calls, cycles, reads, writes, **kw):
        def fn(e):
            last = None
            for c in calls:
                last = c(e)
            return last
        return add({"pe": (fn, cycles * pec)}, reads, writes, **kw)

    def mm(out, lhsT, rhs, start, stop):
        return lambda e: e.matmul(out, lhsT, rhs, start, stop)

    def tr(out, in_, idn):
        return lambda e: e.transpose(out, in_, idn)

    def diag(ap, n, pattern, base, value, rng):
        return pool(lambda e: e.affine_select(ap, ap, pattern, A.not_equal, value, base, 1), n, [rng], [rng])

    def iota(ap, n, pattern, base, rng, step=0):
        return pool(lambda e: e.iota(ap, pattern, base, step, allow_small_or_imprecise_dtypes=True), n, [], [rng])

    prev = {"sy": [], "ac": []}

    def dma(q, dst, src, reads, writes, sem, lat=1.7, after=(), in_turn=True):
        prev[q].append(add({q: (lambda e: e.dma_start(dst, src), 0.06)}, reads, writes, sem, 16, after, lat, prev[q][-1:] if in_turn else ()))

    def loads(gate, after):
        for n, (name, when, lat) in enumerate(CFG["loads"]):
            if when != gate:
                continue
            sem = "d_l%d" % n
            if name in ("th0", "nb0", "th1", "nb1"):
                h, c = int(name[2]), 8 * int(name[2]) + 4 * (name[:2] == "nb")
                dma("sy", T.raw[:, c:c + 4, :], T[name[:2]][:, 128 * h:128 * h + 128], [], [("raw", c, c + 4)], sem, lat, after)
                for a in range(4 if name[:2] == "nb" else 0):
                    lo = 256 * h + 64 * a
                    vec(lambda e, h=h, a=a, lo=lo: e.tensor_copy(T.num[:, lo:lo + 64], T.raw[:, 8 * h:8 * h + 8, 8 * a:8 * a + 8]),
                        64, [("raw", 8 * h, 8 * h + 8)], [("num", lo, lo + 64)], name="nu%d" % a)
            elif name in ("tb0", "tb1"):
                h = int(name[2])
                dma("sy", T.tbr[:, 4 * h:4 * h + 4, :], T.tb[:, 128 * h:128 * h + 128], [], [("tbr", 4 * h, 4 * h + 4)], sem, lat, after)
                for a in range(4):
                    c = 128 * h + 32 * a
                    vec(lambda e, h=h, a=a, c=c: e.tensor_scalar(T.tbf[:, c:c + 32], T.tbr[:, 4 * h:4 * h + 4, 8 * a:8 * a + 8],
                                                                 16.0, 16.0 * 593, A.mult, A.add),
                        32, [("tbr", 4 * h, 4 * h + 4)], [("tbf", c, c + 32)], name="tb%d" % a)
            elif name in ("own0", "own1"):
                lo = 512 * int(name[3])
                dma("sy", T.ownb[:, lo:lo + 512], T.own[:, lo:lo + 512], [], [("ownb", lo, lo + 512)], sem, lat, after)
            else:
                dma("sy", T.tab[:, name[0]:name[1]], T.pair[:, name[0]:name[1]], [], [("tab",) + name], sem, lat, after)

    def remote(k, src, dst, reads, writes, name, lat, behind):
        to = T.cores[(rank + k + 1) % nr]
        rid, pid, _ = topo.addr(to)

        def call(e):
            e.remote_dma_fused([RemoteDMATransfer(dst_ids=[DstId(rid=rid, pnc=pid)], dma_engine_mask=topo.mask(core, to),
                                                  remote_sem=T.sem["arr" + name], src=src, dst=dst)], local_sem=T.sem["loc" + name])

        s = add({"gp": (call, CFG["issue"])}, reads, [], "loc" + name, len(topo.engines(core, to)), (), lat - 0.3, behind)
        add({"far": (None, 0.0)}, [], writes, "arr" + name, len(topo.engines(T.cores[(rank - k - 1) % nr], core)), [s], 0.3 - CFG["hop"])
        return s

    dma("sy", T.stc[96:128, :], T.st[:], [], [("stc", 0, 256)], "d_st")
    dma("ac", T.sdr[:], T.sd[:], [], [("sdr", 0, 64)], "d_sd")
    loads(None, ())

    vec(lambda e: e.memset(T.stb[:], 0.0), 128, [], [("stb", 0, 256)])
    vec(lambda e: e.memset(T.seln[:], 0.0), 256, [], [("seln", 0, 512)])
    vec(lambda e: e.memset(T.sel3[:], 0.0), 12, [], [("sel3", 0, 24)])
    vec(lambda e: e.memset(T.stb[0:1, :], 1.0), 128, [], [("stb", 0, 256, 0, 1)])
    iota(T.stb[64:65, :], 256, [[1, 256]], 0, ("stb", 0, 256, 64, 65))
    diag(T.seln[96:128, :, :, R_STATE], 32, [[-1, 4], [-4, 8]], 0, 1.0, ("seln", 0, 512, 96, 128))
    iota(T.seln[0:1, :, :, R_HI], 32, [[256, 4], [0, 8]], 1024 * rank, ("seln", 0, 512, 0, 1))
    vec(lambda e: e.memset(T.seln[64:65, :, :, R_LO], 1.0), 16, [], [("seln", 0, 512, 64, 65)])
    diag(T.sel3[:], 24, [[-16, 8], [-1, 3]], -R_LO, 1.0, ("sel3", 0, 24))
    vec(lambda e: e.tensor_scalar(T.stb[96:128, :], T.stc[96:128, :], -16.0, None, A.add), 256, [("stc", 0, 256)], [("stb", 0, 256, 96, 128)])
    vec(lambda e: e.tensor_copy(T.sdo[:], T.sdr[:]), 64, [("sdr", 0, 64)], [("sdo", 0, 64)])
    for j in range(4):
        bank = "pa%d" % j
        pe([mm(T[bank][:, 0:256], T.seln[:, j, :, :], T.stb[:], True, True)], 256, [("seln", 0, 512), ("stb", 0, 256)], [(bank, 0, 256)])
        copy(both, T.M[:, 256 * j:256 * j + 256], T[bank][:, 0:256], 256, False, [(bank, 0, 256)], [("M", 256 * j, 256 * j + 256)])

    sent = []
    for k in range(nr - 1):
        d, bank, lo = (rank + k + 1) % nr, ("px0", "px1", "pa0")[k], 48 * k
        for e2 in range(2):
            gather("xs", 256 * k + 128 * e2, 128, "M", 1024, "sdo", 16 * d + 8 * e2)
        pe([mm(T[bank][:, 24 * e2:24 * e2 + 24], T.xs[:, 256 * k + 128 * e2:256 * k + 128 * e2 + 128], T.sel3[:], True, True) for e2 in range(2)], 128,
           [("xs", 256 * k, 256 * k + 256), ("sel3", 0, 24)], [(bank, 0, 48)])
        packed = copy(both, T.snd0[:, lo:lo + 48], T[bank][:, 0:48], 48, False, [(bank, 0, 48)], [("snd0", lo, lo + 48)])
        sent.append(remote(k, T.snd0[:, lo:lo + 48], T.lnd0[:, lo:lo + 48], [("snd0", lo, lo + 48)], [("lnd0", lo, lo + 48)], "m%d" % k,
                           CFG["first"] + CFG["lat"] + 0.3 * k, sent[-1:]))
        loads("m%d" % k, sent[-1:])
    late = {"behind": [packed]}
    for o in ops:
        if o["name"]:
            o["behind"].append(packed)
    gather("M", 1024 + 256 * rank, 256, "M", 1024, "sdo", 16 * rank)
    w0 = 1024 * rank
    copy(both, T.W[:, w0 + 512:w0 + 1024], T.M[:, 512:1024], 512, True, [("M", 512, 1024)], [("W", w0 + 512, w0 + 1024)], **late)

    vec(lambda e: e.memset(ident, 0.0), 64, [], [("ident", 0, 128)])
    diag(ident, 128, [[-1, 128]], 0, 1.0, ("ident", 0, 128))
    vec(lambda e: e.tensor_copy(idf, ident), 128, [("ident", 0, 128)], [("idf", 0, 128)], **late)
    vec(lambda e: e.memset(T.D[:], 0.0), 216, [], [("D", 0, 3)])
    for m, row, value in ((D_TH, R_STATE, 592.0), (D_NB, R_STATE, 1.0), (D_COL, R_LO, 1.0), (D_COL, R_HI, 1.0)):
        diag(T.D[:, m, 15:128:16], 8, [[-16, 8]], -row, value, ("D", m, m + 1))
    ops[iota(T.pat[:], 256, [[0, 16], [1, 16]], -16, ("pat", 0, 256))]["behind"] = sent[-1:]
    vec(lambda e: e.tensor_scalar(T.rst[:], T.pat[:], -16.0, BIG, A.is_equal, A.mult), 256, [("pat", 0, 256)], [("rst", 0, 256)], **late)
    vec(lambda e: e.memset(T.mb[:, 0:1], 0.0), 1, [], [("mb", 0, 1)], **late)
    vec(lambda e: e.memset(T.padm[:], 0.0), 384, [], [("padm", 0, 3)], **late)
    vec(lambda e: e.memset(T.padw[:], 0.0), 768, [], [("padw", 0, 3)], **late)
    vec(lambda e: e.memset(T.pado[:], 0.0), 256, [], [("pado", 0, 4)], **late)
    iota(T.pado[:, R_LO:512:16], 32, [[0, 2], [128, 2], [0, 8]], 0, ("pado", 0, 4), 1)
    iota(T.pado[:, R_HI:512:16], 32, [[256, 2], [0, 2], [0, 8]], 1024 * rank, ("pado", 0, 4))

    def spread(k, src, rng, h, tag):
        w, name = 1024 * ((rank - k - 1) % nr) + 512 * h, "w%s%d" % (tag, k)
        copy(both, T.padw[:, 512 * k + 15:512 * k + 512:16], src, 32, True, [rng], [("padw", k, k + 1)], name="p%s%d" % (tag, k))
        m = 384 if name in CFG["halves"].split() else 512
        bank, c = ("pra", "prb")[k & 1], 512 * (k // 2)
        if m < 512:
            pe([mm(T.pa2[:, 0:128], T.padw[:, 512 * k + 384:512 * k + 512], ident, True, True)], 128,
               [("padw", k, k + 1), ("ident", 0, 128)], [("pa2", 0, 128)], name="T" + name + "s")
            copy(both, T.W[:, w + m:w + 512], T.pa2[:, 0:128], 128, False, [("pa2", 0, 128)], [("W", w + m, w + 512)], name=name + "s")
        pe([tr(T[bank][:, c + j:c + j + 128], T.padw[:, 512 * k + j:512 * k + j + 128], ident) for j in range(0, m, 128)], m,
           [("padw", k, k + 1), ("ident", 0, 128)], [(bank, c, c + m)], name="T" + name)
        copy(both, T.W[:, w:w + m], T[bank][:, c:c + m], m, True, [(bank, c, c + m)], [("W", w, w + m)], name=name)

    def listed(k, row, src, rng):
        bank, c = ("pra", "prb")[k & 1], 512 * (k // 2)
        w = 1024 + 256 * ((rank - k - 1) % nr)
        copy(both, T.padm[:, 16 * k:16 * k + 16, row:16], src, 48, True, [rng], [("padm", k, k + 1)], name="pm%d" % k)
        pe([tr(T[bank][:, c + 128 * j:c + 128 * j + 128], T.padm[:, 16 * k + 8 * j:16 * k + 8 * j + 8, :], ident) for j in range(2)], 256,
           [("padm", k, k + 1), ("ident", 0, 128)], [(bank, c, c + 256)], name="Twm%d" % k)
        copy(both, T.M[:, w:w + 256], T[bank][:, c:c + 256], 256, True, [(bank, c, c + 256)], [("M", w, w + 256)], name="wm%d" % k)

    for k in range(nr - 1):
        listed(k, R_LO, T.lnd0[:, 48 * k:48 * k + 48], ("lnd0", 48 * k, 48 * k + 48))

    def turn(bank, col, m, x, lo, n, start, stop, **kw):
        return pe([mm(T[bank][:, col:col + n // 16], T.D[:, m, 15 - i:143 - i], T[x][:, lo + i:lo + n:16], start and i == 0, stop and i == 15)
                   for i in range(16)], max(1024, n), [("D", m, m + 1), (x, lo, lo + n)], [(bank, col, col + n // 16)], **kw)

    def compose(n):
        h, c = n // 4, 64 * n
        turn("pa3", c, D_COL, ("xth", "xnb")[n // 2 & 1], 2048 * h + 1024 * (n & 1), 1024, True, True, name="C%d" % n)
        if n & 3 == 3:
            vec(lambda e: e.tensor_copy(T.co[:, 256 * h:256 * h + 256], T.pa3[:, 256 * h:256 * h + 256]), 256,
                [("pa3", 256 * h, 256 * h + 256)], [("co", 256 * h, 256 * h + 256)], name="co%d" % h)

    def offsets(u, a0, na, t):
        h, lo, n, bank = t & 1, 32 * a0, 32 * na, "px%d" % (u & 1)
        x0 = 2048 * min(t, 2)
        for k, x in enumerate(("th", "nb")):
            for a in range(a0, a0 + na):
                if t < 2:
                    gather("x" + x, x0 + 512 * a, 512, "M", 2048, "num", 256 * h + 64 * a + 32 * k, "%s%d" % (x, a))
                else:
                    gather("x" + x, x0 + 512 * a, 512, "W", 4096, "co", 256 * h + 128 * k + 32 * a, "%s%d" % (x, a))
            if k == 0 and t >= CFG["wide"]:
                pe([mm(T[bank][:, 0:n], idf, T.tbf[:, 128 * h + lo:128 * h + lo + n], True, False)], 256,
                   [("idf", 0, 128), ("tbf", 128 * h + lo, 128 * h + lo + n)], [(bank, 0, n)], name="Ttb%d" % u)
            turn(bank, 0, (D_TH, D_NB)[k], "x" + x, x0 + 512 * a0, 512 * na, k == 0 and t < CFG["wide"], k == 1, name="T%s%d" % (x, u))
        if t >= CFG["wide"]:
            vec(lambda e: e.tensor_copy(T.po[:, lo:lo + n], T[bank][:, 0:n]), n, [(bank, 0, n)], [("po", lo, lo + n)], name="po%d" % u)
            return
        vec(lambda e: e.tensor_tensor(T.ia[:, lo:lo + n], T[bank][:, 0:n], T.tbf[:, 128 * h + lo:128 * h + lo + n], A.add), n,
            [(bank, 0, n), ("tbf", 128 * h + lo, 128 * h + lo + n)], [("ia", lo, lo + n)], name="ia%d" % u)
        vec(lambda e: e.tensor_scalar(T.ib[:, lo:lo + n], T.ia[:, lo:lo + n], 8191, None, A.bitwise_and), n,
            [("ia", lo, lo + n)], [("ib", lo, lo + n)], name="ib%d" % u)
        vec(lambda e: e.tensor_copy(T.po[:, lo:lo + n], T.ib[:, lo:lo + n]), n, [("ib", lo, lo + n)], [("po", lo, lo + n)], name="po%d" % u)

    acc = {}
    for n, (a0, na) in enumerate(CFG["low"]):
        for k in range(na):
            acc[a0 + k] = ("pa%d" % n, 128 * k)

    def sums(a, t):
        bank, c = acc[a]
        r = 512 * (t & 1) + 128 * a
        out = T[bank][:, c:c + 128]
        gather("xp", 512 * a, 512, "tab", 17088 if t >= CFG["wide"] else 8192, "po", 32 * a, "xp%d" % a)
        pe([mm(out, T.ownb[:, r:r + 128], ident, True, False)], 128, [("ownb", r, r + 128), ("ident", 0, 128), ("po", 32 * a, 32 * a + 32)],
           [(bank, c, c + 128)], name="So%d" % a)
        for half in range(2):
            lo = 512 * a + 256 * half
            pe([mm(out, T.xp[:, lo + 128 * k:lo + 128 * k + 128], ident, False, half == 1 and k == 1) for k in range(2)], 256,
               [("xp", lo, lo + 256)], [(bank, c, c + 128)], name="S%s%d" % ("ab"[half], a))

    def lowest(a0, na, t):
        bank, c = acc[a0]
        lo, n = 128 * a0, 128 * na
        vec(lambda e: e.tensor_tensor_scan(T.mb[:, lo + 1:lo + n + 1], T.rst[:, 0:n], T[bank][:, c:c + n], 0.0, A.add, A.min), n,
            [(bank, c, c + n), ("rst", 0, 256)], [("mb", lo + 1, lo + n + 1)], name="mb%d" % a0)
        vec(lambda e: e.tensor_tensor(T.nd[:, lo:lo + n], T[bank][:, c:c + n], T.mb[:, lo:lo + n], A.is_ge), n,
            [(bank, c, c + n), ("mb", lo, lo + n)], [("nd", lo, lo + n)], name="nd%d" % a0)
        vec(lambda e: e.tensor_tensor_scan(T.cb[:, lo:lo + n], T.nd[:, lo:lo + n], T.pat[:, 0:n], 0.0, A.mult, A.min), n // 2,
            [("nd", lo, lo + n), ("pat", 0, 256)], [("cb", lo, lo + n)], name="cb%d" % a0)
        if 0 < t < ROUNDS - 1:
            s0 = 32 * t + 8 * a0
            copy(both, T.snd[:, s0:s0 + 8 * na], T.cb[:, lo + 15:lo + n:16], 8 * na, True, [("cb", lo, lo + n)], [("snd", s0, s0 + 8 * na)], name="sn%d" % a0)
        if t == 0:
            back = ("pra", "prb")[a0 & 1]
            pe([tr(T[back][:, 128 * a:128 * a + 128], T.cb[:, 128 * a:128 * a + 128], ident) for a in range(a0, a0 + na)], n,
               [("cb", lo, lo + n), ("ident", 0, 128)], [(back, lo, lo + n)], name="Two%d" % a0)
            copy(both, T.W[:, w0 + lo:w0 + lo + n], T[back][:, lo:lo + n], n, True, [(back, lo, lo + n)], [("W", w0 + lo, w0 + lo + n)], name="wo%d" % a0)

    def share_listed():
        sent = []
        for n, c in enumerate((16, 80)):
            copy(both, T.snd1[:, c:c + 32], T.cb[:, 15:512:16], 32, True, [("cb", 0, 512)], [("snd1", c, c + 32)], name="sc%d" % n)
        for k, (lo, c) in enumerate(((0, 0), (16, 48), (64, 64))):
            d, bank = (rank + k + 1) % nr, ("px0", "px1", "pa2")[k]
            gather("xs", 256 * k, 256, "W", 1024, "sdo", 16 * d, "sd%d" % k, w0)
            pe([mm(T[bank][:, 8 * e2:8 * e2 + 8], T.xs[:, 256 * k + 128 * e2:256 * k + 128 * e2 + 128], T.ident[:, 15:128:16], True, True) for e2 in range(2)],
               128, [("xs", 256 * k, 256 * k + 256), ("ident", 0, 128)], [(bank, 0, 16)], name="Tsl%d" % k)
            copy(both, T.snd1[:, c:c + 16], T[bank][:, 0:16], 16, False, [(bank, 0, 16)], [("snd1", c, c + 16)], name="sl%d" % k)
            sent.append(remote(k, T.snd1[:, lo:lo + 48], T.lnd[:, 48 * k:48 * k + 48], [("snd1", lo, lo + 48)], [("lnd", 48 * k, 48 * k + 48)],
                               "0%d" % k, CFG["lat"] + CFG["row"], sent[-1:]))
        loads("x0", sent[-1:])
        copy(both, T.pado[:, 15:512:16], T.cb[:, 15:512:16], 32, True, [("cb", 0, 512)], [("pado", 0, 4)], name="pp")
        pe([tr(T.prb[:, 512 + 128 * a:640 + 128 * a], T.pado[:, 128 * a:128 * a + 128], ident) for a in range(4)], 512,
           [("pado", 0, 4), ("ident", 0, 128)], [("prb", 512, 1024)], name="Tmo")
        copy(both, T.M[:, 0:512], T.prb[:, 512:1024], 512, True, [("prb", 512, 1024)], [("M", 0, 512)], name="mo")
        gather("M", 1024 + 256 * rank, 256, "M", 1024, "sdo", 16 * rank, "sd3")
        for k in range(nr - 1):
            c = 48 * k + (0, 32, 0)[k]
            listed(k, R_STATE, T.lnd[:, c:c + 16], ("lnd", 48 * k, 48 * k + 48))

    def catch_up():
        for k in range(nr - 1):
            c = 48 * k + (16, 0, 16)[k]
            spread(k, T.lnd[:, c:c + 32], ("lnd", 48 * k, 48 * k + 48), 0, "v")

    def share(t):
        h, sent = t & 1, []
        if CFG["fused"]:
            to = [T.cores[(rank + k + 1) % nr] for k in range(nr - 1)]
            mask = topo.mask(core, to[0]) & topo.mask(core, to[1]) & topo.mask(core, to[2])
            n = bin(mask).count("1")

            def call(e):
                e.remote_dma_fused([RemoteDMATransfer(dst_ids=[DstId(rid=topo.addr(c)[0], pnc=topo.addr(c)[1]) for c in to], dma_engine_mask=mask,
                                                      remote_sem=T.sem["arr%d%d" % (t, rank)], src=T.snd[:, 32 * t:32 * t + 32],
                                                      dsts=[T.lnd[:, 96 * t + 32 * k + 48:96 * t + 32 * k + 80] for k in range(nr - 1)])],
                                   local_sem=T.sem["loc%d0" % t])

            s = add({"gp": (call, CFG["issue"])}, [("snd", 32 * t, 32 * t + 32)], [], "loc%d0" % t, n, (), CFG["lat"])
            for k in range(nr - 1):
                lo = 96 * t + 32 * k + 48
                add({"far": (None, 0.0)}, [], [("lnd", lo, lo + 32)], "arr%d%d" % (t, (rank - k - 1) % nr), n, [s], CFG["row"] * (k + 1) - CFG["hop"])
        for k in range(0 if CFG["fused"] else nr - 1):
            lo = 96 * t + 32 * k + 48
            sent.append(remote(k, T.snd[:, 32 * t:32 * t + 32], T.lnd[:, lo:lo + 32], [("snd", 32 * t, 32 * t + 32)], [("lnd", lo, lo + 32)],
                               "%d%d" % (t, k), CFG["lat"] + CFG["row"] + (CFG["row"] - CFG["issue"]) * k, sent[-1:]))
        w = 1024 * rank + 512 * h
        pe([tr(T.prb[:, 512 + 128 * a:640 + 128 * a], T.cb[:, 128 * a:128 * a + 128], ident) for a in range(4)], 512,
           [("cb", 0, 512), ("ident", 0, 128)], [("prb", 512, 1024)], name="Two")
        copy(both, T.W[:, w:w + 512], T.prb[:, 512:1024], 512, True, [("prb", 512, 1024)], [("W", w, w + 512)], name="wo")
        for k in range(nr - 1):
            lo = 96 * t + 32 * k + 48
            spread(k, T.lnd[:, lo:lo + 32], ("lnd", lo, lo + 32), h, "r")

    def store(a0, na, h, banks):
        lo, n, c = 128 * a0, 128 * na, 512 * h + 128 * a0
        for out, buf, bank, bias in ((T.e, "esb", banks[0], 0.0), (T.y, "ysb", banks[1], 16.0)):
            if bias:
                pe([mm(T[bank][0:8 * na, 0:128], T.cb[:, lo + 15:lo + n:16], ident, True, True)], 128,
                   [("cb", lo, lo + n), ("ident", 0, 128)], [(bank, 0, 128)], name="Ty%d" % a0)
            else:
                pe([tr(T[bank][0:8 * na, 0:128], T.mb[:, lo + 16:lo + n + 1:16], idf)], 512,
                   [("mb", lo + 1, lo + n + 1), ("idf", 0, 128)], [(bank, 0, 128)], name="Te%d" % a0)
            copy(both, T[buf][0:8 * na, c:c + 128], T[bank][0:8 * na, 0:128], 128, False, [(bank, 0, 128)], [(buf, c, c + 128)], bias,
                 name="%s%d" % (buf[:2], a0))
            for a in range(na):
                dma("ac" if bias and a0 == 3 else "sy", out[:, c + 128 * a:c + 128 * a + 128], T[buf][8 * a:8 * a + 8, c:c + 128],
                    [(buf, c, c + 128)], [], "d_out", 1.5, (), False)

    def arrange(start, order):
        named = {o["name"]: n for n, o in enumerate(ops) if n >= start}
        for q, names in order.items():
            line = [named[x] for x in names.split() if x in named]
            for a, b in zip([None] + line, line):
                ops[b]["opt"] = {q: ops[b]["opt"][q]}
                ops[b]["behind"] += [a] if a is not None else []

    for t in range(ROUNDS):
        start = len(ops)
        for u, (a0, na) in enumerate(CFG["units"] if t else ((0, 2), (2, 2))):
            offsets(u, a0, na, t)
        for n, when in enumerate(CFG["comp"]):
            if when == t:
                compose(n)
        for n, (when, lo, m) in enumerate(CFG["again"]):
            if when == t:
                copy(both, T.tab[:, lo:lo + m], T.tab[:, lo % 8192:lo % 8192 + m], m, True, [("tab", lo % 8192, lo % 8192 + m)], [("tab", lo, lo + m)],
                     name="ag%d" % n)
        for a0, na in CFG["low"]:
            for a in range(a0, a0 + na):
                sums(a, t)
            lowest(a0, na, t)
            if t == ROUNDS - 1:
                store(a0, na, 1, (("px0", "px1"), None, ("pa3", "px0"), ("px1", "pa0"))[a0])
        if t == 0:
            share_listed()
        if t == 1:
            catch_up()
        if 0 < t < ROUNDS - 1:
            share(t)
        if t == ROUNDS - 2:
            store(0, 4, 0, ("pa0", "pa1"))
        arrange(start, CFG["ord"][t])
        for o in ops[start:]:
            o["seg"] = t
    emit(g, T, ops, schedule(ops))
